import numpy as np, ml_dtypes
CORES = [35,38,43,46]
N = 4
BF = ml_dtypes.bfloat16
def gentries(a):
    return np.ascontiguousarray(a.reshape(8, 16, -1).transpose(0, 2, 1)).reshape(8, -1)
def gtable(e):
    e = np.asarray(e); return np.ascontiguousarray(e.reshape(8, -1, 16).transpose(0, 2, 1)).reshape(128, -1).astype(np.int32)
V, G, D, S, RO = 2048, 512, 2, 16, 3
def parts(rng):
    o = np.argsort(rng.random((N, 8, V)), axis=2); pos = np.argsort(o, axis=2)
    x = rng.integers(0, 256, (N, 8, 16, 1)) + np.add.accumulate(rng.integers(-100, 101, (N, 8, 16, V)), axis=3)
    phi = np.take_along_axis(x, pos[:, :, None, :], 3) & 255
    nb = np.stack([np.take_along_axis(o, (pos + j) % V, 2) for j in (-1, 1, -32, 32)[:D]], 2)
    snd = np.argsort(rng.random((N, 8, V)), axis=2)[..., :G]
    return phi, nb, np.ascontiguousarray(snd)
def mix(rng, nb, own, ghost):
    z = rng.random(nb.shape)
    nb = np.where(z < ghost, rng.integers(V, V + G, nb.shape), np.where(z < ghost + own, rng.integers(0, V, nb.shape), nb))
    return np.take_along_axis(nb, np.argsort(rng.random(nb.shape), axis=2), 2)
def pack(phi, nb, snd):
    return {"phi": np.ascontiguousarray(phi.reshape(N, 128, V)).astype(np.float32).astype(BF), "nb": np.ascontiguousarray(nb.reshape(N, 8, D * V)).astype(np.int32),
            "snd": np.stack([gtable(a) for a in snd])}
def setup_inputs(rng):
    phi, nb, snd = parts(rng)
    own = rng.choice(np.array([0.0, 0.05, 0.15, 0.3]), (N, 8, 1, 1)); ghost = rng.choice(np.array([0.02, 0.05, 0.1, 0.2]), (N, 8, 1, 1))
    return pack(phi, mix(rng, nb, own, ghost), snd)
def setup_inputs_chains(rng):
    phi, nb, snd = parts(rng); v = np.arange(V); lens = [S, S + 1, S + 2, 2 * S + 1, 3 * S, S * S + 1, V, 5]
    steep = rng.random((N, 8, 16, 1)) < 0.5; steep[np.arange(N), (6 - np.arange(N)) % 8, :8] = True
    step = np.where(steep, rng.choice(np.array([-1, 1]), (N, 8, 16, 1)) * rng.integers(100, 128, (N, 8, 16, V)), rng.integers(-100, 101, (N, 8, 16, V)) + rng.integers(-27, 28, (N, 8, 16, 1)))
    phi = (rng.integers(0, 256, (N, 8, 16, 1)) + np.add.accumulate(step, axis=3)) & 255
    for q in range(N):
        for g in range(8):
            b = lens[(g + q) % 8]; head = v - v % b
            down = np.maximum(v - 1, head); up = np.minimum(np.minimum(v + 1, head + b - 1), V - 1)
            nb[q, g] = np.stack([down, up, v, down][:D])
            h = v[v % b == 0][1::2]; nb[q, g, D - 1, h] = rng.integers(V, V + G, len(h))
    return pack(phi, mix(rng, nb, 0.0, 0.0), snd)
def steep_sums(rng, n):
    return np.concatenate([np.zeros((16, 1), np.int64), np.add.accumulate(rng.integers(122, 128, (16, n)), axis=1)], axis=1)
def deep(rng, phi, nb, snd, g):
    T = S * (S + 1); t = np.arange(T + 1); root = t % (S + 1) == 0; slot = rng.integers(0, G, N); last = np.zeros((N, 16, 1), np.int64)
    sign = np.where(np.argsort(rng.random((N, 16, 1)), axis=1) < 8, 1, -1)
    for q in range(N):
        w = np.sort(rng.permutation(V // 2)[:T + 1]); a = np.zeros(T + 1, np.int64)
        a[root] = w[:S + 1]; a[~root] = w[S + 1:]
        y = rng.integers(0, 256, (16, 1)) + sign[q] * steep_sums(rng, T)
        phi[q, g][:, a] = y & 255; last[q] = y[:, T:] & 255
        lo = np.concatenate([a[:1], a[:-1]]); nb[q, g][:, a] = np.stack([lo, a, lo, a][:D]); snd[q, g, slot[q]] = a[T]
    for q in range(N):
        w = V // 2 + np.sort(rng.permutation(V // 2)[:(S + 1) * (S + 1)]); o = (q - 1) % N
        b = np.zeros(T + 1, np.int64); b[0] = V + slot[o]
        b[1:][root[1:]] = np.concatenate([w[:S - 1], w[2 * S:2 * S + 1]]); b[1:][~root[1:]] = w[2 * S + 1:]
        y = last[o] + sign[o] * steep_sums(rng, T); phi[q, g][:, b[1:]] = y[:, 1:] & 255
        nb[q, g][:, b[1:]] = np.stack([b[:-1], b[1:], b[:-1], b[1:]][:D])
        z = w[S - 1:2 * S]; y = rng.integers(0, 256, (16, 1)) - sign[o] * steep_sums(rng, S); phi[q, g][:, z] = y & 255
        lo = np.concatenate([z[S:], z[:-1]]); hi = np.concatenate([z[S:], z[1:S], b[T:]])
        nb[q, g][:, z] = np.stack([lo, hi, lo, hi][:D])
def late(rng, nb, g):
    J = 3 * S; F = J + 2; P = S * S + S + 1; M = 3 * F + P + 4; j = np.arange(F)
    path = np.concatenate([np.array([J - 1]), 3 * F + np.arange(S), 3 * F + np.arange(S + 1, P), np.array([M - 1])])
    lo = np.arange(M); hi = np.arange(M)
    lo[:F] = F + j; hi[:F] = F + j; lo[J:F] = j[J:]
    lo[F:2 * F] = j; hi[F + 1:2 * F] = 2 * F + j[:-1]; lo[2 * F:3 * F] = j
    lo[path[1:]] = path[:-1]
    c = 3 * F + S; lo[c] = M - 4; hi[c] = M - 4; lo[M - 4] = M - 1; hi[M - 4] = M - 1
    lo[M - 3] = M - 2; hi[M - 3] = M - 2; lo[M - 2] = M - 3; hi[M - 2] = M - 1
    for q in range(N):
        w = np.sort(rng.permutation(V)[:M]); nb[q, g][:, w] = np.stack([w[lo], w[hi], w[lo], w[hi]][:D])
def setup_inputs_loops(rng):
    phi, nb, snd = parts(rng); nb = mix(rng, nb, 0.1, rng.choice(np.array([0.02, 0.05, 0.1]), (N, 8, 1, 1)))
    far = S * S; J = min(S + 2, V // (1 + S + far)); M = J * (1 + S + far)
    ids = np.sort(np.argsort(rng.random((N, 8, V)), axis=2)[..., :M], axis=2)
    j = np.arange(J).reshape(J, 1); br = J + S * j + np.arange(S); pa = J + J * S + far * j + np.arange(far)
    lo = np.concatenate([br[:, S - 1], np.concatenate([j, br[:, :-1]], axis=1).reshape(-1), np.concatenate([j, pa[:, :-1]], axis=1).reshape(-1)])
    hi = np.arange(M); hi[:J] = br[:, S - 1]; hi[br[1:, S - 1]] = pa[:-1, far - 1]
    step = rng.choice(np.array([-1, 1]), (N, 8, 16, 1, 1)) * rng.integers(120, 128, (N, 8, 16, J, S + far)); a = rng.integers(0, 256, (N, 8, 16, J, 1))
    xb = a - np.add.accumulate(step[..., :S], axis=4); xp = a + np.add.accumulate(step[..., S:], axis=4)
    x = np.concatenate([a.reshape(N, 8, 16, J), xb.reshape(N, 8, 16, J * S), xp.reshape(N, 8, 16, J * far)], axis=3) & 255
    for q in range(N):
        for g in (0, 1, 3, 4, 6, 7):
            w = ids[q, g]; phi[q, g][:, w] = x[q, g]
            nb[q, g][:, w] = np.stack([w[lo], w[hi], w[lo], w[hi]][:D])
    deep(rng, phi, nb, snd, 2); late(rng, nb, 5)
    return pack(phi, mix(rng, nb, 0.0, 0.0), snd)
def setup_inputs_ties(rng):
    phi, nb, snd = parts(rng); v = np.arange(V)
    t = rng.choice(np.array([0, 1, 127, 128, 129, 255]), (N, 8, 16, 6)); phi = np.take_along_axis(t, rng.integers(0, 6, (N, 8, 1, V)), 3)
    nb = mix(rng, nb, 0.2, rng.choice(np.array([0.0, 0.05, 0.15]), (N, 8, 1, 1)))
    nb[:, 1::2, 1] = nb[:, 1::2, 0]; nb[:, 2, 0] = v
    nb[:, 4] = np.minimum(v + rng.integers(0, 5, (N, D, V)), V - 1)
    return pack(phi, nb, snd)
def setup_inputs_ring(rng):
    phi, nb, snd = parts(rng)
    share = np.stack([rng.permutation(np.array([0.0, 0.0, 0.3, 0.3, 0.7, 0.7, 1.0, 1.0])) for q in range(N)]).reshape(N, 8, 1, 1)
    nb = mix(rng, nb, 0.1 * (share < 0.9), share)
    snd[:, ::2] = rng.choice(np.array([0, V - 1, V // 2, 3]), (N, 4, G)); snd[:, 1, 0] = 0; snd[:, 1, G - 1] = V - 1
    nb[:, 3] = rng.choice(np.array([0, V - 1, V, V + G - 1]), (N, D, V))
    top = V - V // 16; snd[:, 5] = rng.integers(top, V, (N, G))
    high = np.where(rng.random((N, D, V)) < 0.5, rng.integers(V, V + G, (N, D, V)), rng.integers(top, V, (N, D, V)))
    nb[:, 5] = np.where(np.arange(V) < top, high, rng.integers(0, 16, (N, D, V)))
    return pack(phi, nb, snd)
def setup_inputs_spread(rng):
    phi, nb, snd = parts(rng)
    phi = np.minimum((np.exp2(8 * rng.random((N, 8, 1, V))) * rng.random((N, 8, 16, V))).astype(np.int64), 255)
    hub = np.minimum(((V + G) * rng.random(nb.shape) ** 3).astype(np.int64), V + G - 1)
    nb = mix(rng, np.where(rng.random(nb.shape) < rng.choice(np.array([0.1, 0.3, 0.6]), (N, 8, 1, 1)), hub, nb), 0.0, 0.05)
    snd = np.minimum((V * rng.random((N, 8, G)) ** 2).astype(np.int64), V - 1)
    return pack(phi, nb, snd)
def check_inputs(d):
    bad = []
    for k, lo, hi in (("phi", 0, 255), ("nb", 0, V + G - 1), ("snd", 0, V - 1)):
        a = np.asarray(d[k]).astype(np.float64)
        if not (np.min(a) >= lo and np.max(a) <= hi): bad.append("range of " + k)
    a = np.asarray(d["phi"]).astype(np.float64)
    if not np.all(a == np.floor(a)): bad.append("whole numbers in phi")
    return bad
def narrow(t, ix):
    return np.take_along_axis(t, ix, 2)
def broad(t, ix):
    return np.take_along_axis(t, ix[:, :, None, :], 3)
def absolute(r, k, gk, gb):
    gh = r >= V; c = np.where(gh, r - V, 0)
    return k + np.where(gh[:, :, None, :], broad(gk, c), 0), np.where(gh, narrow(gb, c), N * r + np.arange(N).reshape(N, 1, 1))
def reference(phi, nb, snd):
    p = phi.astype(np.float32).astype(np.int64).reshape(N, 8, 16, V); nbl = nb.astype(np.int64).reshape(N, 8, D, V)
    sl = np.stack([gentries(a) for a in snd]).astype(np.int64); before = (np.arange(N) - 1) % N
    own = np.zeros((N, 8, V), np.int64) + np.arange(V); slot = np.zeros((N, 8, G), np.int64) + np.arange(V, V + G)
    num = N * own + np.arange(N).reshape(N, 1, 1); none = np.zeros((N, 8, 16, G), np.int64); BIG = 2 ** 40
    r, k, s = own.copy(), np.zeros((N, 8, 16, V), np.int64), own.copy(); ks, b = k.copy(), num.copy()
    gp = broad(p, sl)[before]
    for rnd in range(RO):
        gk, gb = broad(ks, sl)[before], narrow(b, sl)[before]
        ks, b = absolute(r, k, gk, gb)
        uw = np.concatenate([p + 256 * ks, gp + 256 * gk], axis=3); bw = np.concatenate([b, gb], axis=2)
        rw = np.concatenate([r, slot], axis=2); kw = np.concatenate([k, none], axis=3); sw = np.concatenate([ks, gk], axis=3)
        us = broad(uw, s); cj = np.full((N, 8, V), BIG); cw = cj.copy(); uj = np.zeros((N, 8, V), np.int64); ww = uj.copy()
        for i in range(D):
            u = narrow(nbl[:, :, i], s); c = np.add.reduce(np.abs(broad(uw, u) - us), axis=2)
            t = (narrow(bw, u) < num) & (c < cj); cj = np.where(t, c, cj); uj = np.where(t, u, uj)
            t = (narrow(rw, u) == own) & (c < cw); cw = np.where(t, c, cw); ww = np.where(t, u, ww)
        root = r == own; join = root & (cj < BIG)
        o = ((broad(uw, uj) - us + 128) >> 8) + broad(kw, uj) - broad(sw, uj)
        pw = np.concatenate([np.where(join, narrow(rw, uj), r), slot], axis=2)
        ow = np.concatenate([np.where(join[:, :, None, :], o, k), none], axis=3)
        s = np.where(root & ~join & (cw < BIG), ww, s)
        r, k = own.copy(), np.zeros((N, 8, 16, V), np.int64)
        for step in range(S):
            k = k + broad(ow, r); r = narrow(pw, r)
        ks, b = absolute(r, k, gk, gb)
    return {"yk": ks.reshape(N, 128, V).astype(np.float32), "yr": b.astype(np.float32)}

@@ -1,0 +1,420 @@
+from concourse.bass import DstId, RemoteDMATransfer
+from concourse.mybir import AluOpType, ActivationFunctionType
+
+V, G, W = 2048, 512, 2560
+H = V // 2
+QN = V // 4
+WD = W + 2 * V
+F32, BF, I32, U16, F16 = "float32", "bfloat16", "int32", "uint16", "float16"
+
+
+def _sb(n, d):
+    return ("sbuf", [128, n], d)
+
+
+SCRATCH = {
+    "phiw": _sb(W, BF), "phis": _sb(V, BF), "dw1": _sb(WD, BF), "u2": _sb(WD, F32), "u3": _sb(WD, F32),
+    "ki": _sb(W, I32), "ka": _sb(W, F32), "kb": _sb(W, F32), "tt": _sb(V, F32), "us": _sb(V, F32),
+    "ab0": _sb(V, F32), "ab1": _sb(V, F32), "kd": _sb(V, I32),
+    "nbw": _sb(V, I32), "un": _sb(V, F16), "yy": _sb(WD, BF),
+    "z0": _sb(W, BF), "z1": _sb(W, BF), "z2": _sb(W, BF), "z3": _sb(V, BF),
+    "wd2": _sb(G + 16, BF), "wd3": _sb(G + 16, F32),
+    "sp": _sb(G, BF), "sk2": _sb(G, BF), "sk3": _sb(G, F32), "su2": _sb(G, F32), "su3": _sb(G, F32),
+    "sm": _sb(G, BF), "sb2": _sb(G, BF), "sb3": _sb(G, BF), "posg": _sb(G, BF), "cm": _sb(QN, BF),
+    "sndi": _sb(32, I32), "snl": _sb(32, U16), "spi": _sb(32, I32), "spl": _sb(32, U16),
+    "nl": _sb(256, I32), "nl2": _sb(256, F32), "nl3": _sb(256, F32),
+    "ul": _sb(256, U16), "ul2": _sb(256, U16), "uf": _sb(256, F32), "du0": _sb(128, F32), "d10": _sb(128, F32),
+    "bl": _sb(128, U16), "pl0": _sb(128, U16), "pl1": _sb(128, U16), "ll": _sb(128, U16), "lg": _sb(128, U16),
+    "sl": _sb(128, U16), "vw": _sb(128, F32), "pw": _sb(128, F32), "lf": _sb(128, F32),
+    "rt": _sb(128, BF), "nr": _sb(256, F32),
+    "e0": _sb(128, BF), "e1": _sb(128, BF), "dm": _sb(128, BF), "ds": _sb(128, BF), "dj": _sb(128, BF), "dr": _sb(128, BF),
+    "dy": _sb(128, BF), "dz": _sb(128, BF), "dx": _sb(128, F32), "q0": _sb(128, BF), "q1": _sb(128, BF),
+    "sy": _sb(128, F32), "sz": _sb(128, F32), "ts0": _sb(128, F32), "ts1": _sb(128, F32), "yrs": _sb(128, F32),
+    "xg": _sb(8, I32), "x18": _sb(8, F32), "x2": _sb(8, I32), "x16": _sb(8, I32), "pi": _sb(4, I32), "pf": _sb(4, F32),
+    "j4": _sb(4, F32), "eq": _sb(4, F32), "q4": _sb(2, F32), "abc": _sb(2, F32), "cc": _sb(1, F32), "cq": _sb(1, F32),
+    "m0": _sb(1, F32), "m23": _sb(1, F32), "h64": _sb(40, F32), "at": _sb(40, F32), "ata": _sb(40, F32), "atb": _sb(40, F32),
+    "lo64": _sb(64, F32), "pa": _sb(16, F32), "pb": _sb(16, F32), "pau": _sb(16, U16), "pbu": _sb(16, U16), "c16": _sb(128, F32),
+    "one": _sb(128, F32), "idf": _sb(128, F32), "idb": _sb(128, BF),
+    "rpm": _sb(64, F32), "fp": _sb(144, BF), "fb": _sb(144, BF), "f0": _sb(144, F16), "f1": _sb(144, F16),
+    "zf": _sb(144, F32), "gob": _sb(8, BF), "gof": _sb(8, F32), "neg": _sb(3, F32),
+    "phip": ("psum", [128, V], F32), "dec0": ("psum", [128, 512], F32), "dec1": ("psum", [128, 512], F32),
+    "tp0": ("psum", [128, 512], F32), "tp1": ("psum", [128, 512], F32),
+}
+NDMA = 72
+SEQ = ["d00 n00 d10 n10 a00 a10 c0 d01 d11 n01 r e0 a01 a11 c1 j0 n11 v0 e1 s0 j1 v1 s1"] * 3
+GS = [256]
+SEMAPHORES = ["cv", "cs", "cp", "cg", "sent"] + ["d%d" % i for i in range(NDMA)] + ["a%d" % i for i in range(8)]
+A = AluOpType
+ACT = ActivationFunctionType
+
+
+def rank_program(g, core, T, topo):
+    rank = T.rank_of(core)
+    if rank is None:
+        return
+    n = len(T.cores)
+    nxt, prv = T.cores[(rank + 1) % n], T.cores[(rank - 1) % n]
+    assert topo.may_write(core, nxt)
+    rid, pid = topo.addr(nxt)[:2]
+    eng_out, eng_in = topo.engines(core, nxt), topo.engines(prv, core)
+    Q = {"v": g.vector, "s": g.scalar, "p": g.tensor, "g": g, "y": g.sync}
+    CS = {"v": "cv", "s": "cs", "p": "cp", "g": "cg"}
+    count = {}
+    seen = {q: {} for q in Q}
+    hist = {}
+    ndma = [0]
+
+    def ap(name, lo=0, hi=None, step=None):
+        if hi is None:
+            hi = SCRATCH[name][1][1]
+        a = T[name][:, lo:hi] if step is None else T[name][:, lo:hi:step]
+        return (a, [(name, lo, hi)])
+
+    def ind(win, off):
+        return (win[0].indirect(off[0]), win[1] + off[1])
+
+    def need(q, sem, val):
+        if seen[q].get(sem, 0) < val:
+            Q[q].wait_ge(T.sem[sem], val)
+            seen[q][sem] = val
+
+    def order(q, reads, writes):
+        want = {}
+        for rs, w in ((reads, False), (writes, True)):
+            for name, lo, hi in rs:
+                psum = SCRATCH[name][0] == "psum"
+                for l2, h2, w2, q2, sem, val in hist.get(name, []):
+                    if (psum and q2 != q) or ((w or w2) and l2 < hi and lo < h2):
+                        want[sem] = max(want.get(sem, 0), val)
+        for sem in want:
+            need(q, sem, want[sem])
+
+    def note(q, reads, writes, sem, val):
+        for rs, w in ((reads, False), (writes, True)):
+            for name, lo, hi in rs:
+                h = hist.setdefault(name, [])
+                if w:
+                    h[:] = [x for x in h if not (lo <= x[0] and x[1] <= hi)]
+                h.append((lo, hi, w, q, sem, val))
+
+    def regs(xs):
+        out = []
+        for x in xs:
+            if isinstance(x, tuple):
+                out += x[1]
+        return out
+
+    def raw(x):
+        return x[0] if isinstance(x, tuple) else x
+
+    def run(q, out, ins, calls, each=False, wait=True):
+        r, w = regs(ins), out[1]
+        order(q, r, w if wait else [])
+        sem = CS[q]
+        for i, c in enumerate(calls):
+            inst = c()
+            if each or i == len(calls) - 1:
+                inst.then_inc(T.sem[sem], 1)
+                count[sem] = count.get(sem, 0) + 1
+        note(q, r, w, sem, count[sem])
+
+    def cp(out, x):
+        run("v", out, [x], [lambda: g.vector.tensor_copy(out[0], x[0])])
+
+    def tt(out, x, y, op):
+        run("v", out, [x, y], [lambda: g.vector.tensor_tensor(out[0], x[0], y[0], op)])
+
+    def ts(out, x, s1, op0, s2=None, op1=None):
+        if op1 is None:
+            run("v", out, [x, s1], [lambda: g.vector.tensor_scalar(out[0], x[0], raw(s1), None, op0)])
+        else:
+            run("v", out, [x, s1, s2], [lambda: g.vector.tensor_scalar(out[0], x[0], raw(s1), raw(s2), op0, op1)])
+
+    def ms(out, c):
+        run("v", out, [], [lambda: g.vector.memset(out[0], c)])
+
+    def act(out, x, func=ACT.Identity, **kw):
+        k2 = {k: raw(kw[k]) for k in kw}
+        run("s", out, [x] + list(kw.values()), [lambda: g.scalar.activation(out[0], x[0], func, **k2)])
+
+    def iota(out, pattern, base, cm):
+        if SCRATCH[out[1][0][0]][2] == I32:
+            run("g", out, [], [lambda: g.iota(out[0], pattern, base, cm)])
+        else:
+            run("g", out, [], [lambda: g.iota(out[0], pattern, base, cm, allow_small_or_imprecise_dtypes=True)])
+
+    def dma(q, out, x):
+        r, w = regs([x]), regs([out])
+        order(q, r, w)
+        sem = "d%d" % ndma[0]
+        ndma[0] += 1
+        Q[q].dma_start(raw(out), raw(x)).then_inc(T.sem[sem], 16)
+        count[sem] = 16
+        note(q, r, w, sem, 16)
+
+    def twin(dst, src, lo, hi):
+        m = lo + GS[0]
+        if m > lo:
+            run("g", ap(dst, lo, m), [ap(src, lo, m)],
+                [lambda: g.affine_select(T[dst][:, lo:m], T[src][:, lo:m], [[0, m - lo]], A.is_ge, 0.0, 0, 0)])
+        if m < hi:
+            dma("y", ap(dst, m, hi), ap(src, m, hi))
+
+    def send(src, dst, sem):
+        order("g", src[1], [])
+        g.remote_dma(dst[0], src[0], T.sem[sem], T.sem.sent, pid, rid, topo.mask(core, nxt))
+        count["sent"] = count.get("sent", 0) + len(eng_out)
+        count[sem] = len(eng_in)
+        note("r", [], dst[1], sem, len(eng_in))
+
+    def extract(out, sel, src, lo, hi):
+        run("p", out, [ap(sel), ap(src, lo, hi)],
+            [lambda i=i: g.tensor.matmul(out[0], T[sel][:, 15 - i:143 - i], T[src][:, lo + i:hi:16], i == 0, i == 15) for i in range(16)])
+
+    dma("y", ap("sndi"), T.snd[:])
+    dma("s", ap("phiw", 0, H), T.phi[:, 0:H])
+    dma("y", ap("phiw", H, V), T.phi[:, H:V])
+    dma("s", ap("nl", 0, 128), T.nb[0:8:2, :])
+    dma("y", ap("nl", 128, 256), T.nb[1:8:2, :])
+    dma("y", ap("z1", 0, V), T.phi[:, :])
+    iota(ap("xg"), [[-16, 8]], 0, 1)
+    iota(ap("j4"), [[1, 4]], 0, 0)
+    iota(ap("h64"), [[64, 40]], 0, 0)
+    iota(ap("lo64"), [[1, 64]], 0, 0)
+    iota(ap("pa"), [[16, 8], [128, 2]], 0, 0)
+    iota(ap("pb"), [[2, 16]], 0, 0)
+    send(ap("sndi"), ap("spi"), "a1")
+    ms(ap("fp"), 0.0)
+    ms(ap("fb"), 0.0)
+    ms(ap("neg", 0, 1), -0.5)
+    ms(ap("neg", 1, 2), -1.0)
+    ms(ap("neg", 2, 3), float(rank + 1))
+    ts(ap("pi", 0, 1), ap("xg", 0, 1), 15, A.bitwise_and)
+    ts(ap("pi", 1, 2), ap("xg", 0, 1), 7, A.bitwise_and)
+    cp(ap("pf", 0, 2), ap("pi", 0, 2))
+    ts(ap("x2"), ap("xg"), 1, A.arith_shift_right)
+    ts(ap("eq"), ap("j4"), ap("pf", 0, 1), A.is_equal)
+    ts(ap("x16"), ap("xg"), 4, A.arith_shift_right)
+    ts(ap("q4"), ap("eq", 2, 4), 4.0, A.mult)
+    ts(ap("cc"), ap("eq", 3, 4), float(rank + 1), A.mult)
+    tt(ap("abc"), ap("q4"), ap("eq", 0, 2), A.add)
+    ts(ap("m0"), ap("eq", 0, 1), float(V), A.mult)
+    ts(ap("at"), ap("h64"), ap("abc", 0, 1), A.mult)
+    ts(ap("yy", 0, 64), ap("lo64"), ap("abc", 1, 2), A.mult, ap("cc"), A.add)
+    ts(ap("cq"), ap("eq", 3, 4), float((rank - 1) % n + 1), A.mult)
+    ts(ap("atb"), ap("h64"), ap("q4", 0, 1), A.mult)
+    cp(ap("snl"), ap("sndi"))
+    ts(ap("z0", 0, 64), ap("lo64"), ap("q4", 1, 2), A.mult, ap("cq"), A.add)
+    ts(ap("ata"), ap("h64"), ap("eq", 0, 1), A.mult)
+    ts(ap("posg", 0, 64), ap("lo64"), ap("eq", 1, 2), A.mult, ap("m0"), A.add)
+    for k in range(5):
+        ts(ap("z0", 64 << k, 128 << k), ap("z0", 0, 64 << k), ap("atb", 1 << k, (1 << k) + 1), A.add)
+        if k < 3:
+            ts(ap("posg", 64 << k, 128 << k), ap("posg", 0, 64 << k), ap("ata", 1 << k, (1 << k) + 1), A.add)
+        if k == 3:
+            ts(ap("pau"), ap("pa"), ap("pf", 0, 1), A.add)
+    for k in range(5):
+        if k == 3:
+            act(ap("sp"), ind(ap("phiw", 0, V), ap("snl")))
+            send(ap("sp"), ap("phiw", V, W), "a0")
+        act(ap("yy", 64 << k, 128 << k), ap("yy", 0, 64 << k), bias=ap("at", 1 << k, (1 << k) + 1))
+    ts(ap("pf", 2, 3), ap("pf", 1, 2), 31.875, A.mult)
+    cp(ap("nl2"), ind(ap("nl"), ap("pau")))
+    ts(ap("pf", 3, 4), ap("pf", 0, 1), 0.125, A.mult, ap("pf", 2, 3), A.add)
+    run("v", ap("nl3"), [ap("nl2")], [lambda: g.vector.transpose(T.nl3[:, :], T.nl2[:, :])])
+    ts(ap("pbu"), ap("pb"), ap("pf", 3, 4), A.add)
+    cp(ap("spl"), ap("spi"))
+    cp(ap("ul"), ind(ap("nl3"), ap("pbu")))
+    tt(ap("yy", V, W), ind(ap("z0", 0, V), ap("spl")), ap("posg"), A.add)
+    ts(ap("fb", 15, 143, 16), ap("x2"), 1.0, A.is_equal)
+    ts(ap("gob"), ap("x16"), 0.0, A.is_equal, 2.0 ** -13, A.mult)
+    iota(ap("c16"), [[16, 128]], 0, 0)
+    act(ap("vw"), ap("c16"), bias=ap("pf", 0, 1))
+    for j in range(4):
+        act(ap("nr", 64 * j, 64 * j + 64), ap("vw", 64 * (j // 2), 64 * (j // 2) + 64), scale=4.0, bias=ap("neg", 2, 3))
+    iota(ap("one"), [[0, 128]], 1, 0)
+    run("g", ap("idf"), [ap("one")], [lambda: g.affine_select(T.idf[:, :], T.one[:, :], [[-1, 128]], A.is_equal, 0.0, 0, 1)])
+    iota(ap("cm"), [[0, QN]], -128, 0)
+    act(ap("idb"), ap("idf"), scale=1.0 / 256)
+    calls = []
+    for j in range(4):
+        calls += [lambda j=j: g.tensor.matmul(T.phip[:, QN * j:QN * j + QN], T.idb[:, :], T.phiw[:, QN * j:QN * j + QN], True, False),
+                  lambda j=j: g.tensor.matmul(T.phip[:, QN * j:QN * j + QN], T.idb[:, :], T.cm[:, :], False, True)]
+    run("p", ap("phip"), [ap("idb"), ap("cm"), ap("phiw", 0, V)], calls, each=True)
+    for name, lo, hi in (("dw1", 0, W), ("ki", V, W), ("ka", V, W), ("kb", V, W), ("wd2", 0, 16), ("wd3", 0, 16), ("zf", 0, 144)):
+        iota(ap(name, lo, hi), [[0, hi - lo]], 0, 0)
+    iota(ap("x18"), [[-18, 8]], 0, 1)
+    dma("y", ap("z0", V, W), ap("yy", V, W))
+
+    def load_rows():
+        sem = "d%d" % ndma[0]
+        ndma[0] += 1
+        for j in range(8):
+            g.sync.dma_start(T.nbw[16 * j:16 * j + 16, :], T.nb[:]).then_inc(T.sem[sem], 16)
+        count[sem] = 128
+        note("y", [], ap("nbw")[1], sem, 128)
+
+    load_rows()
+
+    for rnd in range(3):
+        x = "z%d" % rnd
+        znext = "z%d" % (rnd + 1)
+        uw = ("phiw", "u2", "u3")[rnd]
+        dw = ("dw1", "u2", "u3")[rnd]
+        in1 = ("z1", "phis", "us")[rnd]
+        ul = ("ul", "ul", "ul2")[rnd]
+        ab = (("z2", "z3"), ("ab0", "ab1"), ("ab0", "ab1"))[rnd]
+        go = ("gob", "gof", "gof")[rnd]
+        if rnd > 0:
+            act(ap("yy", 0, V), ind(ap(x), ap("ll")))
+            dma("y", ap("yy", V, W), ap(x, V, W))
+            for h in range(2):
+                tt(ap(uw, H * h, H * h + H), ind(ap("wd%d" % (rnd + 1)), ap("lg", 64 * h, 64 * h + 64)), ap("tt", H * h, H * h + H), A.add)
+                if rnd == 2:
+                    ts(ap("ul2", 128 * h, 128 * h + 128), ap("tp%d" % h, 0, 128), 1280.0, A.add)
+
+        def col(k, h):
+            return W + V * k + H * h
+
+        def dk(k, h):
+            l0 = 128 * k + 64 * h
+            tt(ap(dw, col(k, h), col(k, h) + H), ind(ap(uw, 0, W), ap(ul, l0, l0 + 64)), ap(in1, H * h, H * h + H), A.subtract)
+
+        def nk(k, h):
+            lo, l0 = col(k, h), 128 * k + 64 * h
+            act(ap("yy", lo, lo + H), ind(ap("yy", 0, W), ap(ul, l0, l0 + 64)))
+            extract(ap("dec%d" % h, 64 * k, 64 * k + 64), "fb", "yy", lo, lo + H)
+
+        def absk(k, h):
+            act(ap(ab[h], H * k, H * k + H), ap(dw, col(k, h), col(k, h) + H), ACT.Abs)
+
+        def cost1(h):
+            tp = "tp%d" % h
+            run("p", ap(tp, 0, 128), [ap(ab[h], 0, V), ap(go)],
+                [lambda i=i: g.tensor.matmul(T[tp][:, i:128:16], T[ab[h]][:, i:V:16], T[go][:, :], True, True) for i in range(16)], each=True)
+
+        def cost2(h):
+            cp(ap("ts%d" % h), ap("tp%d" % h, 0, 128))
+            run("p", ap("dec%d" % h, 128, 192), [ap("ts%d" % h), ap("rpm")],
+                [lambda: g.tensor.matmul(T["dec%d" % h][:, 128:192], T["ts%d" % h][:, :], T.rpm[:, :], True, True)])
+
+        def roots():
+            if rnd > 0:
+                tt(ap("rt"), ap("pw"), ap("vw"), A.is_equal)
+            else:
+                tt(ap("rpm"), ap("idf", 0, 64), ap("idf", 64, 128), A.subtract)
+                ts(ap("fp", 15, 143, 16), ap("x2"), 0.0, A.is_equal)
+                tt(ap("m23"), ap("eq", 2, 3), ap("eq", 3, 4), A.add)
+
+        def decide(h):
+            e, d = "e%d" % h, "dec%d" % h
+            c = (64 * h, 64 * h + 64)
+            tt(ap(e), ap(d, 0, 128), ap("nr", 128 * h, 128 * h + 128), A.is_lt)
+            tt(ap("dm", *c), ap(e, 0, 64), ap(e, 64, 128), A.subtract)
+            tt(ap("dj", *c), ap(e, 0, 64), ap(e, 64, 128), A.max)
+            tt(ap("ds", *c), ap(d, 128, 192), ap("dm", *c), A.is_gt)
+            if rnd > 0:
+                tt(ap("dr", *c), ap("dj", *c), ap("rt", *c), A.mult)
+            ts(ap("dy", *c), ap("ds", *c), float(V), A.mult, float(W), A.add)
+            tt(ap("dz", *c), ap("dy", *c), ap("dr" if rnd else "dj", *c), A.mult)
+            tt(ap("dx", *c), ap("dz", *c), ap("vw", *c), A.add)
+            cp(ap("bl", *c), ap("dx", *c))
+
+        def picks(h):
+            act(ap(x, H * h, H * h + H), ind(ap("yy"), ap("bl", 64 * h, 64 * h + 64)))
+            extract(ap("dec%d" % h, 192, 256), "fp", x, H * h, H * h + H)
+
+        def pickv(h):
+            for lo in (H * h, H * h + QN):
+                b = ap("bl", lo // 16, (lo + QN) // 16)
+                if rnd == 0:
+                    ts(ap("ki", lo, lo + QN), ind(ap(dw), b), 0.5, A.add, 1.0 / 256, A.mult)
+                else:
+                    ts(ap("ki", lo, lo + QN), ind(ap(dw), b), 1.0 / 512, A.add)
+                twin("kd", "ki", lo, lo + QN)
+
+        steps = {"d": dk, "n": nk, "a": absk, "c": cost1, "e": cost2, "j": decide, "v": pickv, "s": picks, "r": roots}
+        for w in SEQ[rnd].split():
+            steps[w[0]](*[int(z) for z in w[1:]])
+        ksrc = ["ki", "ka", "kb", "ka", "kb"]
+        nsrc = [x, "yy", x, "yy", znext]
+        cp(ap("pl0", 0, 64), ap("dec0", 192, 256))
+        for t in range(4):
+            pl = "pl%d" % (t % 2)
+            last = rnd == 2 and t == 3
+            for h in range(2):
+                if not last:
+                    act(ap(nsrc[t + 1], H * h, H * h + H), ind(ap(nsrc[t], 0, W), ap(pl, 64 * h, 64 * h + 64)))
+                    extract(ap("dec%d" % h, 192, 256), "fp", nsrc[t + 1], H * h, H * h + H)
+                else:
+                    for lo, hi in ((0, H),) if h == 0 else ((H, H + 768), (H + 768, V)):
+                        act(ap("z3", lo, hi), ind(ap(nsrc[t], 0, W), ap(pl, lo // 16, hi // 16)))
+                        run("p", ap("tp0", 0, 128), [ap("fb"), ap("z3", lo, hi)],
+                            [lambda i=i: g.tensor.matmul(T.tp0[:, 0:128], T.fb[:, 15 - i:143 - i], T.z3[:, 128 * i:128 * i + 128], i == 0, i == 15)
+                             for i in range(lo // 128, hi // 128)], wait=lo == 0)
+                cuts = [0, QN, 3 * QN // 2, H] if last and h == 1 else [0, QN, H]
+                for j in range(len(cuts) - 1):
+                    lo, hi = H * h + cuts[j], H * h + cuts[j + 1]
+                    if j == 1 and (h == 0 or t < 3):
+                        cp(ap("pl%d" % ((t + h) % 2), 64 - 64 * h, 128 - 64 * h), ap("dec%d" % (1 - h), 192, 256))
+                    tt(ap(ksrc[t + 1], lo, hi), ind(ap(ksrc[t]), ap(pl, lo // 16, hi // 16)), ap("tt" if t else "kd", lo, hi), A.add)
+                    if t < 3:
+                        twin("tt", ksrc[t + 1], lo, hi)
+                    if last:
+                        dma("y", T.yk[:, lo:hi], ap(ksrc[t + 1], lo, hi))
+        if rnd == 2:
+            break
+        sk, sb, su = "sk%d" % (rnd + 2), "sb%d" % (rnd + 2), "su%d" % (rnd + 2)
+        wd, un = "wd%d" % (rnd + 2), "u%d" % (rnd + 2)
+        sems = ["a%d" % (2 + 3 * rnd + j) for j in range(3)]
+        act(ap("sm"), ind(ap(znext, 0, V), ap("snl")), scale=ap("m23"))
+        if rnd == 0:
+            cp(ap(sk), ind(ap("kb", 0, V), ap("snl")))
+        else:
+            tt(ap(sk), ind(ap("kb", 0, V), ap("snl")), ap("sk2"), A.subtract)
+        send(ap(sk), ap(wd, 16, 16 + G), sems[0])
+        tt(ap(sb), ap("sm"), ap("posg"), A.add)
+        send(ap(sb), ap(znext, V, W), sems[1])
+        if rnd == 0:
+            act(ap("phis"), ap("phiw", 0, V), scale=1.0 / 256, bias=ap("neg", 0, 1))
+        else:
+            for h in range(2):
+                c = (64 * h, 64 * h + 64)
+                tt(ap("q0", *c), ap("dec%d" % h, 0, 64), ap("nr", 128 * h, 128 * h + 64), A.is_equal)
+                tt(ap("q1", *c), ap("dec%d" % h, 64, 128), ap("nr", 128 * h, 128 * h + 64), A.is_equal)
+            tt(ap("dm"), ap("q0"), ap("q1"), A.subtract)
+            tt(ap("dj"), ap("q0"), ap("q1"), A.max)
+            for h in range(2):
+                c = (64 * h, 64 * h + 64)
+                tt(ap("ds", *c), ap("dec%d" % h, 128, 192), ap("dm", *c), A.is_gt)
+            tt(ap("sy"), ap("ds"), ap("d10"), A.mult)
+            tt(ap("sz"), ap("sy"), ap("du0"), A.add)
+            tt(ap("sy"), ap("sz"), ap("dj"), A.mult)
+            tt(ap("dx"), ap("sy"), ap("vw"), A.add)
+            cp(ap("sl"), ap("dx"))
+            act(ap("us"), ind(ap("u2", 0, V), ap("sl")))
+        tt(ap("tt"), ap("phip"), ap("kb", 0, V), A.add)
+        act(ap(su), ind(ap("tt"), ap("snl")))
+        send(ap(su), ap(un, V, W), sems[2])
+        for h in range(2):
+            cp(ap("pw", 64 * h, 64 * h + 64), ap("dec%d" % h, 192, 256))
+        tt(ap("lf"), ap("pw"), ap("vw"), A.max)
+        ts(ap("lg"), ap("pw"), float(V - 16), A.subtract, 0.0, A.max)
+        cp(ap("ll"), ap("lf"))
+        if rnd == 1:
+            ts(ap("un"), ind(ap("nbw"), ap("sl")), 1280.0, A.subtract)
+            for k in range(2):
+                extract(ap("tp%d" % k, 0, 128), "f%d" % k, "un", 0, V)
+        else:
+            ts(ap("gof"), ap("x16"), 0.0, A.is_equal, 2.0 ** -15, A.mult)
+            cp(ap("uf"), ap("ul"))
+            cp(ap("f0"), ap("zf"))
+            cp(ap("f1"), ap("zf"))
+            tt(ap("du0"), ap("uf", 0, 128), ap("vw"), A.subtract)
+            tt(ap("d10"), ap("uf", 128, 256), ap("uf", 0, 128), A.subtract)
+            ts(ap("f0", 15, 143, 16), ap("x18"), 0.0, A.is_equal)
+            ts(ap("f1", 15, 143, 16), ap("x18"), 1.0, A.is_equal)
+    act(ap("yrs"), ap("tp0", 0, 128), bias=ap("neg", 1, 2))
+    dma("s", T.yr[:], ap("yrs"))
+    for sem in count:
+        need("g", sem, count[sem])

@@ -5,7 +5,9 @@ V, G, W = 2048, 512, 2560
 H = V // 2
 QN = V // 4
 WD = W + 2 * V
-F32, BF, I32, U16, F16 = "float32", "bfloat16", "int32", "uint16", "float16"
+BIG = 2.0 ** 38
+UNIT = 2.0 ** 21
+F32, BF, I32, U16 = "float32", "bfloat16", "int32", "uint16"
 
 
 def _sb(n, d):
@@ -13,36 +15,38 @@ def _sb(n, d):
 
 
 SCRATCH = {
-    "phiw": _sb(W, BF), "phis": _sb(V, BF), "dw1": _sb(WD, BF), "u2": _sb(WD, F32), "u3": _sb(WD, F32),
-    "ki": _sb(W, I32), "ka": _sb(W, F32), "kb": _sb(W, F32), "tt": _sb(V, F32), "us": _sb(V, F32),
-    "ab0": _sb(V, F32), "ab1": _sb(V, F32), "kd": _sb(V, I32),
-    "nbw": _sb(V, I32), "un": _sb(V, F16), "yy": _sb(WD, BF),
-    "z0": _sb(W, BF), "z1": _sb(W, BF), "z2": _sb(W, BF), "z3": _sb(V, BF),
+    "phr": _sb(V, BF), "phw": _sb(W, BF), "phs": _sb(V, BF), "w1": _sb(WD, BF), "w2": _sb(WD, F32), "w3": _sb(WD, F32),
+    "ki": _sb(W, I32), "ka": _sb(W, F32), "kb": _sb(W, F32), "tt": _sb(V, F32), "kd": _sb(V, I32),
+    "us": _sb(V, F32), "uo": _sb(V, F32), "ab0": _sb(V, F32), "ab1": _sb(V, F32), "ac0": _sb(V, BF), "ac1": _sb(V, BF),
+    "yy": _sb(WD, BF), "z0": _sb(W, BF), "z1": _sb(W, BF), "z2": _sb(W, BF), "z3": _sb(V, BF),
     "wd2": _sb(G + 16, BF), "wd3": _sb(G + 16, F32),
-    "sp": _sb(G, BF), "sk2": _sb(G, BF), "sk3": _sb(G, F32), "su2": _sb(G, F32), "su3": _sb(G, F32),
-    "sm": _sb(G, BF), "sb2": _sb(G, BF), "sb3": _sb(G, BF), "posg": _sb(G, BF), "cm": _sb(QN, BF),
-    "sndi": _sb(32, I32), "snl": _sb(32, U16), "spi": _sb(32, I32), "spl": _sb(32, U16),
-    "nl": _sb(256, I32), "nl2": _sb(256, F32), "nl3": _sb(256, F32),
-    "ul": _sb(256, U16), "ul2": _sb(256, U16), "uf": _sb(256, F32), "du0": _sb(128, F32), "d10": _sb(128, F32),
-    "bl": _sb(128, U16), "pl0": _sb(128, U16), "pl1": _sb(128, U16), "ll": _sb(128, U16), "lg": _sb(128, U16),
-    "sl": _sb(128, U16), "vw": _sb(128, F32), "pw": _sb(128, F32), "lf": _sb(128, F32),
-    "rt": _sb(128, BF), "nr": _sb(256, F32),
-    "e0": _sb(128, BF), "e1": _sb(128, BF), "dm": _sb(128, BF), "ds": _sb(128, BF), "dj": _sb(128, BF), "dr": _sb(128, BF),
-    "dy": _sb(128, BF), "dz": _sb(128, BF), "dx": _sb(128, F32), "q0": _sb(128, BF), "q1": _sb(128, BF),
-    "sy": _sb(128, F32), "sz": _sb(128, F32), "ts0": _sb(128, F32), "ts1": _sb(128, F32), "yrs": _sb(128, F32),
-    "xg": _sb(8, I32), "x18": _sb(8, F32), "x2": _sb(8, I32), "x16": _sb(8, I32), "pi": _sb(4, I32), "pf": _sb(4, F32),
-    "j4": _sb(4, F32), "eq": _sb(4, F32), "q4": _sb(2, F32), "abc": _sb(2, F32), "cc": _sb(1, F32), "cq": _sb(1, F32),
-    "m0": _sb(1, F32), "m23": _sb(1, F32), "h64": _sb(40, F32), "at": _sb(40, F32), "ata": _sb(40, F32), "atb": _sb(40, F32),
+    "sp": _sb(G, BF), "sk2": _sb(G, BF), "sk3": _sb(G, F32), "ou": _sb(G, F32), "f1": _sb(G, BF), "e8": _sb(G, BF),
+    "sm1": _sb(G, BF), "sm2": _sb(G, BF), "sm3": _sb(G, BF), "posg": _sb(G, BF),
+    "sndi": _sb(32, I32), "snl": _sb(32, U16), "el": _sb(32, U16),
+    "nl": _sb(256, I32), "nl2": _sb(256, F32), "nl3": _sb(256, F32), "nh": _sb(256, BF), "nlo": _sb(256, BF),
+    "ul": _sb(256, U16), "ul2": _sb(256, U16), "bl": _sb(256, U16),
+    "pl0": _sb(128, U16), "pl1": _sb(128, U16), "ll": _sb(128, U16), "lg": _sb(128, U16),
+    "vw": _sb(128, F32), "vw2": _sb(256, F32), "top": _sb(256, F32), "nr": _sb(128, F32), "nq": _sb(128, F32),
+    "lf": _sb(128, F32), "rt": _sb(128, BF),
+    "ea0": _sb(256, BF), "ea1": _sb(256, BF), "bs": _sb(256, F32), "bt": _sb(256, F32), "by": _sb(256, F32), "bz": _sb(256, F32),
+    "ts0": _sb(128, F32), "ts1": _sb(128, F32), "yrs": _sb(128, F32),
+    "xj": _sb(8, I32), "ya": _sb(2, I32), "yb": _sb(8, I32), "yc": _sb(1, I32), "xg": _sb(8, I32), "x2": _sb(8, I32), "x16": _sb(8, I32),
+    "x8": _sb(8, I32), "pf": _sb(4, F32), "eq": _sb(8, F32), "abc": _sb(2, F32), "cc": _sb(1, F32),
+    "m0": _sb(1, F32), "m23": _sb(1, F32), "h64": _sb(17, F32), "at": _sb(17, F32), "ata": _sb(17, F32),
     "lo64": _sb(64, F32), "pa": _sb(16, F32), "pb": _sb(16, F32), "pau": _sb(16, U16), "pbu": _sb(16, U16), "c16": _sb(128, F32),
-    "one": _sb(128, F32), "idf": _sb(128, F32), "idb": _sb(128, BF),
-    "rpm": _sb(64, F32), "fp": _sb(144, BF), "fb": _sb(144, BF), "f0": _sb(144, F16), "f1": _sb(144, F16),
-    "zf": _sb(144, F32), "gob": _sb(8, BF), "gof": _sb(8, F32), "neg": _sb(3, F32),
-    "phip": ("psum", [128, V], F32), "dec0": ("psum", [128, 512], F32), "dec1": ("psum", [128, 512], F32),
-    "tp0": ("psum", [128, 512], F32), "tp1": ("psum", [128, 512], F32),
+    "one": _sb(128, F32), "oneb": _sb(64, BF), "idf": _sb(128, F32), "idb": _sb(128, BF), "idn": _sb(128, BF), "idp": _sb(128, BF),
+    "rpm": _sb(64, F32), "fp": _sb(144, BF), "fb": _sb(144, BF), "f0": _sb(144, BF), "f5": _sb(144, BF),
+    "gob": _sb(24, BF), "gof": _sb(8, F32), "neg": _sb(3, F32),
+    "sd": ("dram", [4, 8, V], BF),
+    "dec0": ("psum", [128, 512], F32), "dec1": ("psum", [128, 512], F32), "tp0": ("psum", [128, 512], F32), "tp1": ("psum", [128, 512], F32),
+    "pp0": ("psum", [128, 512], F32), "pp1": ("psum", [128, 512], F32), "xa": ("psum", [128, 512], F32), "xb": ("psum", [128, 512], F32),
 }
-NDMA = 72
-SEQ = ["d00 n00 d10 n10 a00 a10 c0 d01 d11 n01 r e0 a01 a11 c1 j0 n11 v0 e1 s0 j1 v1 s1"] * 3
-GS = [256]
+NDMA = 90
+SEQ = ["d00 n00 n10 d10 d01 a00 d11 e0 a10 r1 c0 t0 n01 c1 n11 j0 v0 e1 t1 s0 j1 s1 v1",
+       "d00 n00 d10 n10 d01 A00 A01 d11 A02 A03 e0 t0 n01 A10 A11 N11 A12 j0 A13 v0 e1 t1 s0 j1 s1 v1",
+       "d00 n00 d10 n10 d01 A00 A01 d11 A02 A03 e0 t0 n01 A10 A11 N11 A12 j0 A13 v0 e1 t1 s0 j1 s1 v1"]
+GS = [0, 512]
+ALT = [1]
 SEMAPHORES = ["cv", "cs", "cp", "cg", "sent"] + ["d%d" % i for i in range(NDMA)] + ["a%d" % i for i in range(8)]
 A = AluOpType
 ACT = ActivationFunctionType
@@ -63,6 +67,7 @@ def rank_program(g, core, T, topo):
     seen = {q: {} for q in Q}
     hist = {}
     ndma = [0]
+    nsend = [0]
 
     def ap(name, lo=0, hi=None, step=None):
         if hi is None:
@@ -143,26 +148,35 @@ def rank_program(g, core, T, topo):
         else:
             run("g", out, [], [lambda: g.iota(out[0], pattern, base, cm, allow_small_or_imprecise_dtypes=True)])
 
-    def dma(q, out, x):
+    def gcopy(out, x):
+        m = out[1][0][2] - out[1][0][1]
+        run("g", out, [x], [lambda: g.affine_select(out[0], x[0], [[0, m]], A.is_ge, 0.0, 0, 0)])
+
+    def dma(q, out, x, **kw):
         r, w = regs([x]), regs([out])
         order(q, r, w)
         sem = "d%d" % ndma[0]
         ndma[0] += 1
-        Q[q].dma_start(raw(out), raw(x)).then_inc(T.sem[sem], 16)
+        Q[q].dma_start(raw(out), raw(x), **kw).then_inc(T.sem[sem], 16)
         count[sem] = 16
         note(q, r, w, sem, 16)
 
-    def twin(dst, src, lo, hi):
-        m = lo + GS[0]
+    def twin(dst, src, lo, hi, j):
+        m = lo + GS[j]
         if m > lo:
-            run("g", ap(dst, lo, m), [ap(src, lo, m)],
-                [lambda: g.affine_select(T[dst][:, lo:m], T[src][:, lo:m], [[0, m - lo]], A.is_ge, 0.0, 0, 0)])
+            gcopy(ap(dst, lo, m), ap(src, lo, m))
         if m < hi:
             dma("y", ap(dst, m, hi), ap(src, m, hi))
 
-    def send(src, dst, sem):
-        order("g", src[1], [])
-        g.remote_dma(dst[0], src[0], T.sem[sem], T.sem.sent, pid, rid, topo.mask(core, nxt))
+    def send(srcs, dst):
+        sem = "a%d" % nsend[0]
+        nsend[0] += 1
+        order("g", regs(srcs), [])
+        if len(srcs) == 1:
+            g.remote_dma(dst[0], srcs[0][0], T.sem[sem], T.sem.sent, pid, rid, topo.mask(core, nxt))
+        else:
+            g.remote_dma_fused([RemoteDMATransfer(dst_ids=[DstId(rid=rid, pnc=pid)], dma_engine_mask=topo.mask(core, nxt), remote_sem=T.sem[sem],
+                                                  srcs=[x[0] for x in srcs], dsts=[dst[0]], alu_op=1)], local_sem=T.sem.sent)
         count["sent"] = count.get("sent", 0) + len(eng_out)
         count[sem] = len(eng_in)
         note("r", [], dst[1], sem, len(eng_in))
@@ -172,249 +186,323 @@ def rank_program(g, core, T, topo):
             [lambda i=i: g.tensor.matmul(out[0], T[sel][:, 15 - i:143 - i], T[src][:, lo + i:hi:16], i == 0, i == 15) for i in range(16)])
 
     dma("y", ap("sndi"), T.snd[:])
-    dma("s", ap("phiw", 0, H), T.phi[:, 0:H])
-    dma("y", ap("phiw", H, V), T.phi[:, H:V])
+    dma("s", ap("phr", 0, H), T.phi[:, 0:H])
+    dma("y", ap("phr", H, V), T.phi[:, H:V])
     dma("s", ap("nl", 0, 128), T.nb[0:8:2, :])
     dma("y", ap("nl", 128, 256), T.nb[1:8:2, :])
-    dma("y", ap("z1", 0, V), T.phi[:, :])
-    iota(ap("xg"), [[-16, 8]], 0, 1)
-    iota(ap("j4"), [[1, 4]], 0, 0)
-    iota(ap("h64"), [[64, 40]], 0, 0)
+    iota(ap("xj"), [[-1, 8]], 16, 1)
+    iota(ap("h64"), [[64, 17]], 0, 0)
     iota(ap("lo64"), [[1, 64]], 0, 0)
+    iota(ap("xg"), [[-16, 8]], 0, 1)
     iota(ap("pa"), [[16, 8], [128, 2]], 0, 0)
     iota(ap("pb"), [[2, 16]], 0, 0)
-    send(ap("sndi"), ap("spi"), "a1")
-    ms(ap("fp"), 0.0)
-    ms(ap("fb"), 0.0)
-    ms(ap("neg", 0, 1), -0.5)
-    ms(ap("neg", 1, 2), -1.0)
-    ms(ap("neg", 2, 3), float(rank + 1))
-    ts(ap("pi", 0, 1), ap("xg", 0, 1), 15, A.bitwise_and)
-    ts(ap("pi", 1, 2), ap("xg", 0, 1), 7, A.bitwise_and)
-    cp(ap("pf", 0, 2), ap("pi", 0, 2))
-    ts(ap("x2"), ap("xg"), 1, A.arith_shift_right)
-    ts(ap("eq"), ap("j4"), ap("pf", 0, 1), A.is_equal)
-    ts(ap("x16"), ap("xg"), 4, A.arith_shift_right)
-    ts(ap("q4"), ap("eq", 2, 4), 4.0, A.mult)
-    ts(ap("cc"), ap("eq", 3, 4), float(rank + 1), A.mult)
-    tt(ap("abc"), ap("q4"), ap("eq", 0, 2), A.add)
-    ts(ap("m0"), ap("eq", 0, 1), float(V), A.mult)
-    ts(ap("at"), ap("h64"), ap("abc", 0, 1), A.mult)
-    ts(ap("yy", 0, 64), ap("lo64"), ap("abc", 1, 2), A.mult, ap("cc"), A.add)
-    ts(ap("cq"), ap("eq", 3, 4), float((rank - 1) % n + 1), A.mult)
-    ts(ap("atb"), ap("h64"), ap("q4", 0, 1), A.mult)
-    cp(ap("snl"), ap("sndi"))
-    ts(ap("z0", 0, 64), ap("lo64"), ap("q4", 1, 2), A.mult, ap("cq"), A.add)
-    ts(ap("ata"), ap("h64"), ap("eq", 0, 1), A.mult)
-    ts(ap("posg", 0, 64), ap("lo64"), ap("eq", 1, 2), A.mult, ap("m0"), A.add)
-    for k in range(5):
-        ts(ap("z0", 64 << k, 128 << k), ap("z0", 0, 64 << k), ap("atb", 1 << k, (1 << k) + 1), A.add)
-        if k < 3:
-            ts(ap("posg", 64 << k, 128 << k), ap("posg", 0, 64 << k), ap("ata", 1 << k, (1 << k) + 1), A.add)
-        if k == 3:
-            ts(ap("pau"), ap("pa"), ap("pf", 0, 1), A.add)
-    for k in range(5):
-        if k == 3:
-            act(ap("sp"), ind(ap("phiw", 0, V), ap("snl")))
-            send(ap("sp"), ap("phiw", V, W), "a0")
-        act(ap("yy", 64 << k, 128 << k), ap("yy", 0, 64 << k), bias=ap("at", 1 << k, (1 << k) + 1))
-    ts(ap("pf", 2, 3), ap("pf", 1, 2), 31.875, A.mult)
-    cp(ap("nl2"), ind(ap("nl"), ap("pau")))
-    ts(ap("pf", 3, 4), ap("pf", 0, 1), 0.125, A.mult, ap("pf", 2, 3), A.add)
-    run("v", ap("nl3"), [ap("nl2")], [lambda: g.vector.transpose(T.nl3[:, :], T.nl2[:, :])])
-    ts(ap("pbu"), ap("pb"), ap("pf", 3, 4), A.add)
-    cp(ap("spl"), ap("spi"))
-    cp(ap("ul"), ind(ap("nl3"), ap("pbu")))
-    tt(ap("yy", V, W), ind(ap("z0", 0, V), ap("spl")), ap("posg"), A.add)
-    ts(ap("fb", 15, 143, 16), ap("x2"), 1.0, A.is_equal)
-    ts(ap("gob"), ap("x16"), 0.0, A.is_equal, 2.0 ** -13, A.mult)
     iota(ap("c16"), [[16, 128]], 0, 0)
-    act(ap("vw"), ap("c16"), bias=ap("pf", 0, 1))
-    for j in range(4):
-        act(ap("nr", 64 * j, 64 * j + 64), ap("vw", 64 * (j // 2), 64 * (j // 2) + 64), scale=4.0, bias=ap("neg", 2, 3))
     iota(ap("one"), [[0, 128]], 1, 0)
     run("g", ap("idf"), [ap("one")], [lambda: g.affine_select(T.idf[:, :], T.one[:, :], [[-1, 128]], A.is_equal, 0.0, 0, 1)])
-    iota(ap("cm"), [[0, QN]], -128, 0)
-    act(ap("idb"), ap("idf"), scale=1.0 / 256)
-    calls = []
+    ms(ap("neg", 0, 1), -0.5)
+    ms(ap("neg", 1, 2), -1.0)
+    ms(ap("neg", 2, 3), (rank + 1) / 4.0)
+    for name in ("fb", "fp", "f0", "f5"):
+        ms(ap(name), 0.0)
+    ts(ap("ya"), ap("xj", 2, 4), 11, A.bitwise_and)
+    ts(ap("yb"), ap("xj"), 15, A.bitwise_and)
+    ts(ap("abc"), ap("ya"), 0.0, A.is_equal)
+    ts(ap("eq"), ap("yb"), 0.0, A.is_equal)
+    ts(ap("cc"), ap("yb", 7, 8), 0.0, A.is_equal, (rank + 1) / 4.0, A.mult)
+    ts(ap("at"), ap("h64"), ap("abc", 0, 1), A.mult)
+    ts(ap("yy", 0, 64), ap("lo64"), ap("abc", 1, 2), A.mult, ap("cc"), A.add)
+    ts(ap("yc"), ap("xj", 0, 1), 7, A.bitwise_and)
+    act(ap("m0"), ap("eq", 2, 3), scale=float(V))
+    act(ap("ata"), ap("h64"), scale=ap("eq", 2, 3))
+    act(ap("m23"), ap("eq", 6, 7), bias=ap("eq", 7, 8))
+    act(ap("posg", 0, 64), ap("lo64"), scale=ap("eq", 3, 4), bias=ap("m0"))
+    for k in range(3):
+        act(ap("posg", 64 << k, 128 << k), ap("posg", 0, 64 << k), bias=ap("ata", 1 << k, (1 << k) + 1))
+    for k in range(5):
+        ts(ap("yy", 64 << k, 128 << k), ap("yy", 0, 64 << k), ap("at", 1 << k, (1 << k) + 1), A.add)
+        if k == 0:
+            cp(ap("pf", 0, 1), ap("yb", 0, 1))
+            cp(ap("pf", 1, 2), ap("yc"))
+        if k == 1:
+            ts(ap("pau"), ap("pa"), ap("pf", 0, 1), A.add)
+            ts(ap("pf", 2, 3), ap("pf", 1, 2), 31.875, A.mult)
+        if k == 2:
+            ts(ap("pf", 3, 4), ap("pf", 0, 1), 0.125, A.mult, ap("pf", 2, 3), A.add)
+            ts(ap("x2"), ap("xg"), 1, A.arith_shift_right)
+        if k == 3:
+            ts(ap("pbu"), ap("pb"), ap("pf", 3, 4), A.add)
+            ts(ap("x16"), ap("xg"), 4, A.arith_shift_right)
+    cp(ap("snl"), ap("sndi"))
+    act(ap("vw"), ap("c16"), bias=ap("pf", 0, 1))
+    act(ap("oneb"), ap("one", 0, 64))
+    act(ap("nr"), ap("vw"), bias=ap("neg", 2, 3))
+    act(ap("sp"), ind(ap("phr"), ap("snl")), scale=1.0 / 256, bias=ap("neg", 0, 1))
+    send([ap("sp")], ap("phw", V, W))
+    act(ap("sm1"), ind(ap("yy", 0, V), ap("snl")), scale=ap("m23"))
+    send([ap("sm1"), ap("posg")], ap("yy", V, W))
+    ts(ap("x8"), ap("xg"), 0x7FF7, A.bitwise_and)
+    ts(ap("fb", 15, 143, 16), ap("x2"), 3.0, A.is_equal)
+    ts(ap("fp", 15, 143, 16), ap("x2"), 1.0, A.is_equal)
+    for j, c in enumerate((UNIT, 2 * UNIT, -UNIT)):
+        ts(ap("gob", 8 * j, 8 * j + 8), ap("x16"), 0.0, A.is_equal, c, A.mult)
+    ts(ap("gof"), ap("x16"), 0.0, A.is_equal, UNIT, A.mult)
+    ts(ap("f0", 15, 143, 16), ap("x8"), 1.0, A.is_equal)
+    ts(ap("f5", 15, 143, 16), ap("x8"), 5.0, A.is_equal)
+    for h in range(2):
+        ts(ap("phw", H * h, H * h + H), ap("phr", H * h, H * h + H), 128.0, A.subtract, 1.0 / 256, A.mult)
+        dma("y", ap("phs", H * h, H * h + H), ap("phw", H * h, H * h + H))
+    cp(ap("nl2"), ind(ap("nl"), ap("pau")))
+    cp(ap("nh"), ap("nl"))
+    run("v", ap("nl3"), [ap("nl2")], [lambda: g.vector.transpose(T.nl3[:, :], T.nl2[:, :])])
+    tt(ap("rpm"), ap("idf", 0, 64), ap("idf", 64, 128), A.subtract)
+    cp(ap("ul"), ind(ap("nl3"), ap("pbu")))
     for j in range(4):
-        calls += [lambda j=j: g.tensor.matmul(T.phip[:, QN * j:QN * j + QN], T.idb[:, :], T.phiw[:, QN * j:QN * j + QN], True, False),
-                  lambda j=j: g.tensor.matmul(T.phip[:, QN * j:QN * j + QN], T.idb[:, :], T.cm[:, :], False, True)]
-    run("p", ap("phip"), [ap("idb"), ap("cm"), ap("phiw", 0, V)], calls, each=True)
-    for name, lo, hi in (("dw1", 0, W), ("ki", V, W), ("ka", V, W), ("kb", V, W), ("wd2", 0, 16), ("wd3", 0, 16), ("zf", 0, 144)):
+        act(ap("vw2", 64 * j, 64 * j + 64), ap("vw", 64 * (j // 2), 64 * (j // 2) + 64))
+    act(ap("idn"), ap("idf"), scale=-BIG)
+    act(ap("idp"), ap("idf"), scale=BIG)
+    act(ap("idb"), ap("idf"))
+    tt(ap("nlo"), ap("nl"), ap("nh"), A.subtract)
+    for h in range(2):
+        ts(ap("top", 128 * h, 128 * h + 128), ap("vw2", 128 * h, 128 * h + 128), float(W + H * h + H), A.add)
+    for name, lo, hi in (("w1", 0, W), ("ki", V, W), ("ka", V, W), ("kb", V, W), ("wd2", 0, 16), ("wd3", 0, 16)):
         iota(ap(name, lo, hi), [[0, hi - lo]], 0, 0)
-    iota(ap("x18"), [[-18, 8]], 0, 1)
     dma("y", ap("z0", V, W), ap("yy", V, W))
-
-    def load_rows():
-        sem = "d%d" % ndma[0]
-        ndma[0] += 1
-        for j in range(8):
-            g.sync.dma_start(T.nbw[16 * j:16 * j + 16, :], T.nb[:]).then_inc(T.sem[sem], 16)
-        count[sem] = 128
-        note("y", [], ap("nbw")[1], sem, 128)
-
-    load_rows()
+    for c in range(4):
+        j0 = 4 * (c // 2) + 2 * (c % 2)
+        dma("y", (T.sd[:, j0:j0 + 2, :], [("sd", j0, j0 + 2)]), ap(("nh", "nlo")[c % 2], 128 * (c // 2), 128 * (c // 2) + 128))
 
     for rnd in range(3):
         x = "z%d" % rnd
         znext = "z%d" % (rnd + 1)
-        uw = ("phiw", "u2", "u3")[rnd]
-        dw = ("dw1", "u2", "u3")[rnd]
-        in1 = ("z1", "phis", "us")[rnd]
+        uw = ("phw", "w2", "w3")[rnd]
+        dw = ("w1", "w2", "w3")[rnd]
         ul = ("ul", "ul", "ul2")[rnd]
-        ab = (("z2", "z3"), ("ab0", "ab1"), ("ab0", "ab1"))[rnd]
-        go = ("gob", "gof", "gof")[rnd]
-        if rnd > 0:
-            act(ap("yy", 0, V), ind(ap(x), ap("ll")))
-            dma("y", ap("yy", V, W), ap(x, V, W))
-            for h in range(2):
-                tt(ap(uw, H * h, H * h + H), ind(ap("wd%d" % (rnd + 1)), ap("lg", 64 * h, 64 * h + 64)), ap("tt", H * h, H * h + H), A.add)
-                if rnd == 2:
-                    ts(ap("ul2", 128 * h, 128 * h + 128), ap("tp%d" % h, 0, 128), 1280.0, A.add)
+        ab = (("ac0", "ac1"), ("ab0", "ab1"), ("ab0", "ab1"))[rnd]
+        go = (ap("gob", 0, 8), ap("gof"), ap("gof"))[rnd]
+        nq = "nq" if rnd else "nr"
+        wide = 128 if rnd == 1 else 64
+        relu = {}
 
         def col(k, h):
-            return W + V * k + H * h
+            return W + V * h + H * k
 
         def dk(k, h):
-            l0 = 128 * k + 64 * h
-            tt(ap(dw, col(k, h), col(k, h) + H), ind(ap(uw, 0, W), ap(ul, l0, l0 + 64)), ap(in1, H * h, H * h + H), A.subtract)
+            l0, lo = 128 * k + 64 * h, col(k, h)
+            w = ind(ap(uw, 0, W), ap(ul, l0, l0 + 64))
+            if rnd == 1:
+                tt(ap(dw, lo, lo + H), w, ap("w1", lo, lo + H), A.add)
+            else:
+                tt(ap(dw, lo, lo + H), w, ap("us" if rnd else "phs", H * h, H * h + H), A.subtract)
 
-        def nk(k, h):
+        def nk(k, h, f=act):
             lo, l0 = col(k, h), 128 * k + 64 * h
-            act(ap("yy", lo, lo + H), ind(ap("yy", 0, W), ap(ul, l0, l0 + 64)))
+            f(ap("yy", lo, lo + H), ind(ap("yy", 0, W), ap(ul, l0, l0 + 64)))
             extract(ap("dec%d" % h, 64 * k, 64 * k + 64), "fb", "yy", lo, lo + H)
 
         def absk(k, h):
             act(ap(ab[h], H * k, H * k + H), ap(dw, col(k, h), col(k, h) + H), ACT.Abs)
 
+        def absq(h, r):
+            lo, tp = col(0, h), "tp%d" % h
+            act(ap(ab[h], QN * r, QN * r + QN), ap(dw, lo + r, lo + V, 4), ACT.Abs)
+            run("p", ap(tp, r, 128), [ap(ab[h], QN * r, QN * r + QN), go],
+                [lambda i=i: g.tensor.matmul(T[tp][:, 4 * i + r:128:16], T[ab[h]][:, QN * r + i:QN * r + QN:4], go[0], True, True) for i in range(4)],
+                each=True, wait=r == 0)
+
+        def pos(h):
+            relu[h] = 1
+            ts(ap(ab[h]), ap(dw, col(0, h), col(0, h) + V), 0.0, A.max)
+
         def cost1(h):
-            tp = "tp%d" % h
-            run("p", ap(tp, 0, 128), [ap(ab[h], 0, V), ap(go)],
-                [lambda i=i: g.tensor.matmul(T[tp][:, i:128:16], T[ab[h]][:, i:V:16], T[go][:, :], True, True) for i in range(16)], each=True)
+            tp, lo = "tp%d" % h, col(0, h)
+            if h not in relu:
+                run("p", ap(tp, 0, 128), [ap(ab[h]), go],
+                    [lambda i=i: g.tensor.matmul(T[tp][:, i:128:16], T[ab[h]][:, i:V:16], go[0], True, True) for i in range(16)], each=True)
+            else:
+                calls = []
+                for i in range(16):
+                    calls += [lambda i=i: g.tensor.matmul(T[tp][:, i:128:16], T[dw][:, lo + i:lo + V:16], T.gob[:, 16:24], True, False),
+                              lambda i=i: g.tensor.matmul(T[tp][:, i:128:16], T[ab[h]][:, i:V:16], T.gob[:, 8:16], False, True)]
+                run("p", ap(tp, 0, 128), [ap(ab[h]), ap(dw, lo, lo + V), ap("gob")], calls, each=True)
+
+        def may(h):
+            e, d, c = "ea%d" % h, "dec%d" % h, ap(nq, 64 * h, 64 * h + 64)
+            for k in range(2):
+                tt(ap(e, 128 * k, 128 * k + 64), ap(d, 64 * k, 64 * k + 64), c, A.is_lt)
+                if rnd == 1:
+                    tt(ap(e, 128 * k + 64, 128 * k + 128), ap(d, 64 * k, 64 * k + 64), c, A.is_le)
+            o = (128 * h, 128 * h + wide)
+            ts(ap("bs", *o), ap(e, 0, wide), float(W + H * h), A.mult)
+            terms = [[("idn", ap("oneb")), ("idn", ap(e, 0, 64)), ("idp", ap(e, 128, 192)), ("idp", ap(e, 128, 192))]]
+            if rnd == 1:
+                terms.append([("idn", ap("oneb")), ("idn", ap(e, 0, 64)), ("idn", ap(e, 64, 128)), ("idp", ap(e, 128, 192)),
+                              ("idp", ap(e, 192, 256)), ("idp", ap(e, 192, 256))])
+            for z, tm in zip((ap(d, 128, 192), ap("pp%d" % h, 128, 192)), terms):
+                run("p", z, [ap("idn"), ap("idp")] + [y[1] for y in tm],
+                    [lambda i=i, z=z, tm=tm: g.tensor.matmul(z[0], T[tm[i][0]][:, :], tm[i][1][0], i == 0, False) for i in range(len(tm))])
+            tt(ap("bt", *o), ap("bs", *o), ap("vw2", *o), A.add)
 
         def cost2(h):
             cp(ap("ts%d" % h), ap("tp%d" % h, 0, 128))
-            run("p", ap("dec%d" % h, 128, 192), [ap("ts%d" % h), ap("rpm")],
-                [lambda: g.tensor.matmul(T["dec%d" % h][:, 128:192], T["ts%d" % h][:, :], T.rpm[:, :], True, True)])
-
-        def roots():
-            if rnd > 0:
-                tt(ap("rt"), ap("pw"), ap("vw"), A.is_equal)
-            else:
-                tt(ap("rpm"), ap("idf", 0, 64), ap("idf", 64, 128), A.subtract)
-                ts(ap("fp", 15, 143, 16), ap("x2"), 0.0, A.is_equal)
-                tt(ap("m23"), ap("eq", 2, 3), ap("eq", 3, 4), A.add)
+            for z in (ap("dec%d" % h, 128, 192), ap("pp%d" % h, 128, 192))[:wide // 64]:
+                run("p", z, [ap("ts%d" % h), ap("rpm")],
+                    [lambda z=z: g.tensor.matmul(z[0], T["ts%d" % h][:, :], T.rpm[:, :], False, True)], wait=False)
 
         def decide(h):
-            e, d = "e%d" % h, "dec%d" % h
-            c = (64 * h, 64 * h + 64)
-            tt(ap(e), ap(d, 0, 128), ap("nr", 128 * h, 128 * h + 128), A.is_lt)
-            tt(ap("dm", *c), ap(e, 0, 64), ap(e, 64, 128), A.subtract)
-            tt(ap("dj", *c), ap(e, 0, 64), ap(e, 64, 128), A.max)
-            tt(ap("ds", *c), ap(d, 128, 192), ap("dm", *c), A.is_gt)
-            if rnd > 0:
-                tt(ap("dr", *c), ap("dj", *c), ap("rt", *c), A.mult)
-            ts(ap("dy", *c), ap("ds", *c), float(V), A.mult, float(W), A.add)
-            tt(ap("dz", *c), ap("dy", *c), ap("dr" if rnd else "dj", *c), A.mult)
-            tt(ap("dx", *c), ap("dz", *c), ap("vw", *c), A.add)
-            cp(ap("bl", *c), ap("dx", *c))
+            o = (128 * h, 128 * h + wide)
+            tt(ap("by", o[0], o[0] + 64), ap("dec%d" % h, 128, 192), ap("bt", o[0], o[0] + 64), A.max)
+            if rnd == 1:
+                tt(ap("by", o[0] + 64, o[1]), ap("pp%d" % h, 128, 192), ap("bt", o[0] + 64, o[1]), A.max)
+            tt(ap("bz", *o), ap("by", *o), ap("top", *o), A.min)
+            cp(ap("bl", *o), ap("bz", *o))
 
         def picks(h):
-            act(ap(x, H * h, H * h + H), ind(ap("yy"), ap("bl", 64 * h, 64 * h + 64)))
-            extract(ap("dec%d" % h, 192, 256), "fp", x, H * h, H * h + H)
+            o = 128 * h + wide - 64
+            act(ap(x, H * h, H * h + H), ind(ap("yy", 0, col(0, h) + V), ap("bl", o, o + 64)))
+            extract(ap("pp%d" % h, 0, 64), "fp", x, H * h, H * h + H)
 
         def pickv(h):
-            for lo in (H * h, H * h + QN):
-                b = ap("bl", lo // 16, (lo + QN) // 16)
-                if rnd == 0:
-                    ts(ap("ki", lo, lo + QN), ind(ap(dw), b), 0.5, A.add, 1.0 / 256, A.mult)
-                else:
-                    ts(ap("ki", lo, lo + QN), ind(ap(dw), b), 1.0 / 512, A.add)
-                twin("kd", "ki", lo, lo + QN)
+            for j in range(2):
+                lo = H * h + QN * j
+                if h == 1 and j == 1:
+                    cp(ap("pl0", 0, 64), ap("pp0", 0, 64))
+                ts(ap("ki", lo, lo + QN), ind(ap(dw, 0, col(0, h) + V), ap("bl", 128 * h + 32 * j, 128 * h + 32 * j + 32)), 1.0 / 512, A.add)
+                twin("kd", "ki", lo, lo + QN, j)
 
-        steps = {"d": dk, "n": nk, "a": absk, "c": cost1, "e": cost2, "j": decide, "v": pickv, "s": picks, "r": roots}
+        steps = {"d": dk, "n": nk, "N": lambda k, h: nk(k, h, cp), "a": absk, "A": absq, "r": pos, "c": cost1, "e": may, "t": cost2,
+                 "j": decide, "v": pickv, "s": picks}
+        if rnd == 1:
+            dma("g", ap("ou"), ap("sp"))
+            dma("g", ap("ou"), ap("sk2"), accum_op=A.add)
         for w in SEQ[rnd].split():
             steps[w[0]](*[int(z) for z in w[1:]])
         ksrc = ["ki", "ka", "kb", "ka", "kb"]
         nsrc = [x, "yy", x, "yy", znext]
-        cp(ap("pl0", 0, 64), ap("dec0", 192, 256))
-        for t in range(4):
-            pl = "pl%d" % (t % 2)
-            last = rnd == 2 and t == 3
-            for h in range(2):
-                if not last:
-                    act(ap(nsrc[t + 1], H * h, H * h + H), ind(ap(nsrc[t], 0, W), ap(pl, 64 * h, 64 * h + 64)))
-                    extract(ap("dec%d" % h, 192, 256), "fp", nsrc[t + 1], H * h, H * h + H)
-                else:
-                    for lo, hi in ((0, H),) if h == 0 else ((H, H + 768), (H + 768, V)):
-                        act(ap("z3", lo, hi), ind(ap(nsrc[t], 0, W), ap(pl, lo // 16, hi // 16)))
-                        run("p", ap("tp0", 0, 128), [ap("fb"), ap("z3", lo, hi)],
-                            [lambda i=i: g.tensor.matmul(T.tp0[:, 0:128], T.fb[:, 15 - i:143 - i], T.z3[:, 128 * i:128 * i + 128], i == 0, i == 15)
-                             for i in range(lo // 128, hi // 128)], wait=lo == 0)
-                cuts = [0, QN, 3 * QN // 2, H] if last and h == 1 else [0, QN, H]
-                for j in range(len(cuts) - 1):
-                    lo, hi = H * h + cuts[j], H * h + cuts[j + 1]
-                    if j == 1 and (h == 0 or t < 3):
-                        cp(ap("pl%d" % ((t + h) % 2), 64 - 64 * h, 128 - 64 * h), ap("dec%d" % (1 - h), 192, 256))
-                    tt(ap(ksrc[t + 1], lo, hi), ind(ap(ksrc[t]), ap(pl, lo // 16, hi // 16)), ap("tt" if t else "kd", lo, hi), A.add)
-                    if t < 3:
-                        twin("tt", ksrc[t + 1], lo, hi)
-                    if last:
-                        dma("y", T.yk[:, lo:hi], ap(ksrc[t + 1], lo, hi))
-        if rnd == 2:
-            break
-        sk, sb, su = "sk%d" % (rnd + 2), "sb%d" % (rnd + 2), "su%d" % (rnd + 2)
-        wd, un = "wd%d" % (rnd + 2), "u%d" % (rnd + 2)
-        sems = ["a%d" % (2 + 3 * rnd + j) for j in range(3)]
-        act(ap("sm"), ind(ap(znext, 0, V), ap("snl")), scale=ap("m23"))
-        if rnd == 0:
-            cp(ap(sk), ind(ap("kb", 0, V), ap("snl")))
-        else:
-            tt(ap(sk), ind(ap("kb", 0, V), ap("snl")), ap("sk2"), A.subtract)
-        send(ap(sk), ap(wd, 16, 16 + G), sems[0])
-        tt(ap(sb), ap("sm"), ap("posg"), A.add)
-        send(ap(sb), ap(znext, V, W), sems[1])
-        if rnd == 0:
-            act(ap("phis"), ap("phiw", 0, V), scale=1.0 / 256, bias=ap("neg", 0, 1))
-        else:
-            for h in range(2):
-                c = (64 * h, 64 * h + 64)
-                tt(ap("q0", *c), ap("dec%d" % h, 0, 64), ap("nr", 128 * h, 128 * h + 64), A.is_equal)
-                tt(ap("q1", *c), ap("dec%d" % h, 64, 128), ap("nr", 128 * h, 128 * h + 64), A.is_equal)
-            tt(ap("dm"), ap("q0"), ap("q1"), A.subtract)
-            tt(ap("dj"), ap("q0"), ap("q1"), A.max)
-            for h in range(2):
-                c = (64 * h, 64 * h + 64)
-                tt(ap("ds", *c), ap("dec%d" % h, 128, 192), ap("dm", *c), A.is_gt)
-            tt(ap("sy"), ap("ds"), ap("d10"), A.mult)
-            tt(ap("sz"), ap("sy"), ap("du0"), A.add)
-            tt(ap("sy"), ap("sz"), ap("dj"), A.mult)
-            tt(ap("dx"), ap("sy"), ap("vw"), A.add)
-            cp(ap("sl"), ap("dx"))
-            act(ap("us"), ind(ap("u2", 0, V), ap("sl")))
-        tt(ap("tt"), ap("phip"), ap("kb", 0, V), A.add)
-        act(ap(su), ind(ap("tt"), ap("snl")))
-        send(ap(su), ap(un, V, W), sems[2])
-        for h in range(2):
-            cp(ap("pw", 64 * h, 64 * h + 64), ap("dec%d" % h, 192, 256))
-        tt(ap("lf"), ap("pw"), ap("vw"), A.max)
-        ts(ap("lg"), ap("pw"), float(V - 16), A.subtract, 0.0, A.max)
-        cp(ap("ll"), ap("lf"))
         if rnd == 1:
-            ts(ap("un"), ind(ap("nbw"), ap("sl")), 1280.0, A.subtract)
-            for k in range(2):
-                extract(ap("tp%d" % k, 0, 128), "f%d" % k, "un", 0, V)
+            extract(ap("xa", 0, 128), "f0", x, 0, V)
+
+        def narrow(t, lo, hi):
+            act(ap(nsrc[t + 1], lo, hi), ind(ap(nsrc[t], 0, W), ap("pl%d" % (t % 2), lo // 16, hi // 16)))
+            extract(ap("pp%d" % (lo // H), lo % H // 16, lo % H // 16 + (hi - lo) // 16), "fp", nsrc[t + 1], lo, hi)
+
+        def broad(t, lo, hi):
+            tt(ap(ksrc[t + 1], lo, hi), ind(ap(ksrc[t]), ap("pl%d" % (t % 2), lo // 16, hi // 16)), ap("tt" if t else "kd", lo, hi), A.add)
+
+        def quarter(t, h, j):
+            return H * h + QN * (j ^ (ALT[0] & (t + 1) & 1))
+
+        def lists(lo, hi, base):
+            p, c = ap("pp%d" % (lo // H), lo % H // 16, lo % H // 16 + (hi - lo) // 16), (lo // 16, hi // 16)
+            tt(ap("lf", *c), p, ap("vw", *c), A.max)
+            ts(ap("lg", *c), p, float(V - 16), A.subtract, 0.0, A.max)
+            ts(ap("ll", *c), ap("lf", *c), float(base), A.subtract)
+
+        def roots(h):
+            c = (64 * h, 64 * h + 64)
+            tt(ap("rt", *c), ap("pp%d" % h, 0, 64), ap("vw", *c), A.is_equal)
+            tt(ap("nq", *c), ap("rt", *c), ap("nr", *c), A.mult)
+
+        for t in range(3):
+            for h in range(2):
+                narrow(t, H * h, H * h + H)
+                if rnd == 1 and t == 0 and h == 0:
+                    extract(ap("xb", 0, 128), "f5", x, 0, V)
+                for j in range(2):
+                    lo = quarter(t, h, j)
+                    if j == 1:
+                        cp(ap("pl%d" % ((t + h) % 2), 64 - 64 * h, 128 - 64 * h), ap("pp%d" % (1 - h), 0, 64))
+                    broad(t, lo, lo + QN)
+                    twin("tt", ksrc[t + 1], lo, lo + QN, j)
+                if rnd == 1 and t == 1:
+                    cp(ap("ul2", 128 * h, 128 * h + 128), ap(("xa", "xb")[h], 0, 128))
+        if rnd == 0:
+            act(ap("e8"), ind(ap("yy", 0, V), ap("snl")))
+            extract(ap("xa", 0, 32), "fp", "e8", 0, G)
+            cp(ap("pl1", 64, 128), ap("pp1", 0, 64))
+            cp(ap("f1"), ind(ap("ka", 0, V), ap("snl")))
+            narrow(3, 3 * QN, V)
+            cp(ap("el"), ap("xa", 0, 32))
+            tt(ap("sk2"), ind(ap("ka"), ap("el")), ap("f1"), A.add)
+            send([ap("sk2")], ap("wd2", 16, 16 + G))
+            act(ap("sm2"), ind(ap("yy", 0, W), ap("el")), scale=ap("m23"))
+            send([ap("sm2"), ap("posg")], ap("z1", V, W))
+            gcopy(ap("w2", V, W), ap("wd2", 16, 16 + G))
+            for j in range(4):
+                q = 3 - j
+                if j:
+                    narrow(3, QN * q, QN * q + QN)
+                dma("y", (T.z1[1:128:4, QN * q:QN * q + QN], [("z1", QN * q, QN * q + QN)]), (T.sd[:, :, QN * q:QN * q + QN], [("sd", 0, 8)]))
+            for j in range(4):
+                lo = quarter(3, j // 2, j % 2)
+                broad(3, lo, lo + QN)
+                if j >= 2:
+                    lists(QN * (5 - j), QN * (6 - j), QN * (5 - j))
+            gcopy(ap("yy", V, W), ap("z1", V, W))
+            for j in range(4):
+                q = 3 - j
+                act(ap("yy", QN * q, QN * q + QN), ind(ap("z1", QN * q, W), ap("ll", 32 * q, 32 * q + 32)))
+                if j == 0:
+                    lists(QN, H, QN)
+                    lists(0, QN, 0)
+                if j % 2 == 0:
+                    h = q // 2
+                    tt(ap("w2", H * h, H * h + H), ind(ap("wd2"), ap("lg", 64 * h, 64 * h + 64)), ap("kb", H * h, H * h + H), A.add)
+                    roots(h)
+        elif rnd == 1:
+            def usum(j):
+                lo, b = quarter(3, j // 2, j % 2), ("xa", "xb")[j % 2]
+                run("p", ap(b), [ap("idb"), ap("idf"), ap("phs", lo, lo + QN), ap("kb", lo, lo + QN)],
+                    [lambda: g.tensor.matmul(T[b][:, :], T.idb[:, :], T.phs[:, lo:lo + QN], True, False),
+                     lambda: g.tensor.matmul(T[b][:, :], T.idf[:, :], T.kb[:, lo:lo + QN], False, True)])
+
+            def uout(j):
+                lo = quarter(3, j // 2, j % 2)
+                act(ap("uo", lo, lo + QN), ap(("xa", "xb")[j % 2]))
+
+            narrow(3, 0, H)
+            broad(3, quarter(3, 0, 0), quarter(3, 0, 0) + QN)
+            usum(0)
+            cp(ap("pl1", 64, 128), ap("pp1", 0, 64))
+            narrow(3, H, V)
+            for j in range(1, 4):
+                lo = quarter(3, j // 2, j % 2)
+                broad(3, lo, lo + QN)
+            usum(1)
+            act(ap("sm3"), ind(ap("z2", 0, V), ap("snl")), scale=ap("m23"))
+            send([ap("sm3"), ap("posg")], ap("z2", V, W))
+            tt(ap("sk3"), ind(ap("kb", 0, V), ap("snl")), ap("sk2"), A.subtract)
+            send([ap("sk3")], ap("wd3", 16, 16 + G))
+            send([ap("sk3"), ap("ou")], ap("w3", V, W))
+            uout(0)
+            usum(2)
+            uout(1)
+            usum(3)
+            uout(2)
+            for h in range(2):
+                lists(H * h, H * h + H, 0)
+                roots(h)
+                tt(ap("us", H * h, H * h + H), ind(ap("w2"), ap("bl", 128 * h + 64, 128 * h + 128)), ap("phs", H * h, H * h + H), A.add)
+            gcopy(ap("yy", V, W), ap("z2", V, W))
+            for h in range(2):
+                act(ap("yy", H * h, H * h + H), ind(ap("z2"), ap("ll", 64 * h, 64 * h + 64)))
+                if h == 0:
+                    uout(3)
+                tt(ap("w3", H * h, H * h + H), ind(ap("wd3"), ap("lg", 64 * h, 64 * h + 64)), ap("uo", H * h, H * h + H), A.add)
         else:
-            ts(ap("gof"), ap("x16"), 0.0, A.is_equal, 2.0 ** -15, A.mult)
-            cp(ap("uf"), ap("ul"))
-            cp(ap("f0"), ap("zf"))
-            cp(ap("f1"), ap("zf"))
-            tt(ap("du0"), ap("uf", 0, 128), ap("vw"), A.subtract)
-            tt(ap("d10"), ap("uf", 128, 256), ap("uf", 0, 128), A.subtract)
-            ts(ap("f0", 15, 143, 16), ap("x18"), 0.0, A.is_equal)
-            ts(ap("f1", 15, 143, 16), ap("x18"), 1.0, A.is_equal)
-    act(ap("yrs"), ap("tp0", 0, 128), bias=ap("neg", 1, 2))
+            for h in range(2):
+                for lo, hi in ((0, H),) if h == 0 else ((H, H + 768), (H + 768, V)):
+                    act(ap("z3", lo, hi), ind(ap("yy", 0, W), ap("pl1", lo // 16, hi // 16)))
+                    run("p", ap("xa", 0, 128), [ap("fb"), ap("z3", lo, hi)],
+                        [lambda i=i: g.tensor.matmul(T.xa[:, 0:128], T.fb[:, 15 - i:143 - i], T.z3[:, 128 * i:128 * i + 128], i == 0, i == 15)
+                         for i in range(lo // 128, hi // 128)], wait=lo == 0)
+                for j in range(2):
+                    lo = quarter(3, h, j)
+                    if j == 1 and h == 0:
+                        cp(ap("pl1", 64, 128), ap("pp1", 0, 64))
+                    for a, b in ((lo, lo + QN // 2), (lo + QN // 2, lo + QN)) if h == 1 and j == 1 else ((lo, lo + QN),):
+                        broad(3, a, b)
+                        dma("y", T.yk[:, a:b], ap("kb", a, b))
+    act(ap("yrs"), ap("xa", 0, 128), scale=4.0, bias=ap("neg", 1, 2))
     dma("s", T.yr[:], ap("yrs"))
     for sem in count:
         need("g", sem, count[sem])

from concourse.bass import DstId, RemoteDMATransfer
from concourse.mybir import AluOpType, ActivationFunctionType

V, G, W = 2048, 512, 2560
H = V // 2
QN = V // 4
WD = W + 2 * V
BIG = 2.0 ** 38
UNIT = 2.0 ** 21
F32, BF, I32, U16 = "float32", "bfloat16", "int32", "uint16"


def _sb(n, d):
    return ("sbuf", [128, n], d)


SCRATCH = {
    "phr": _sb(V, BF), "phw": _sb(W, BF), "phs": _sb(V, BF), "w1": _sb(WD, BF), "w2": _sb(WD, F32), "w3": _sb(WD, F32),
    "ki": _sb(W, I32), "ka": _sb(W, F32), "kb": _sb(W, F32), "tt": _sb(V, F32), "kd": _sb(V, I32),
    "us": _sb(V, F32), "uo": _sb(V, F32), "ab0": _sb(V, F32), "ab1": _sb(V, F32), "ac0": _sb(V, BF), "ac1": _sb(V, BF),
    "yy": _sb(WD, BF), "z0": _sb(W, BF), "z1": _sb(W, BF), "z2": _sb(W, BF), "z3": _sb(V, BF),
    "wd2": _sb(G + 16, BF), "wd3": _sb(G + 16, F32),
    "sp": _sb(G, BF), "sk2": _sb(G, BF), "sk3": _sb(G, F32), "ou": _sb(G, F32), "f1": _sb(G, BF), "e8": _sb(G, BF),
    "sm1": _sb(G, BF), "sm2": _sb(G, BF), "sm3": _sb(G, BF), "posg": _sb(G, BF),
    "sndi": _sb(32, I32), "snl": _sb(32, U16), "el": _sb(32, U16),
    "nl": _sb(256, I32), "nl2": _sb(256, F32), "nl3": _sb(256, F32), "nh": _sb(256, BF), "nlo": _sb(256, BF),
    "ul": _sb(256, U16), "ul2": _sb(256, U16), "bl": _sb(256, U16),
    "pl0": _sb(128, U16), "pl1": _sb(128, U16), "ll": _sb(128, U16), "lg": _sb(128, U16),
    "vw": _sb(128, F32), "vw2": _sb(256, F32), "top": _sb(256, F32), "nr": _sb(128, F32), "nq": _sb(128, F32),
    "lf": _sb(128, F32), "rt": _sb(128, BF),
    "ea0": _sb(256, BF), "ea1": _sb(256, BF), "bs": _sb(256, F32), "bt": _sb(256, F32), "by": _sb(256, F32), "bz": _sb(256, F32),
    "ts0": _sb(128, F32), "ts1": _sb(128, F32), "yrs": _sb(128, F32),
    "xj": _sb(8, I32), "ya": _sb(2, I32), "yb": _sb(8, I32), "yc": _sb(1, I32), "xg": _sb(8, I32), "x2": _sb(8, I32), "x16": _sb(8, I32),
    "x8": _sb(8, I32), "pf": _sb(4, F32), "eq": _sb(8, F32), "abc": _sb(2, F32), "cc": _sb(1, F32),
    "m0": _sb(1, F32), "m23": _sb(1, F32), "h64": _sb(17, F32), "at": _sb(17, F32), "ata": _sb(17, F32),
    "lo64": _sb(64, F32), "pa": _sb(16, F32), "pb": _sb(16, F32), "pau": _sb(16, U16), "pbu": _sb(16, U16), "c16": _sb(128, F32),
    "one": _sb(128, F32), "oneb": _sb(64, BF), "idf": _sb(128, F32), "idb": _sb(128, BF), "idn": _sb(128, BF), "idp": _sb(128, BF),
    "rpm": _sb(64, F32), "fp": _sb(144, BF), "fb": _sb(144, BF), "f0": _sb(144, BF), "f5": _sb(144, BF),
    "gob": _sb(24, BF), "gof": _sb(8, F32), "neg": _sb(3, F32),
    "sd": ("dram", [4, 8, V], BF),
    "dec0": ("psum", [128, 512], F32), "dec1": ("psum", [128, 512], F32), "tp0": ("psum", [128, 512], F32), "tp1": ("psum", [128, 512], F32),
    "pp0": ("psum", [128, 512], F32), "pp1": ("psum", [128, 512], F32), "xa": ("psum", [128, 512], F32), "xb": ("psum", [128, 512], F32),
}
NDMA = 90
SEQ = ["d00 n00 n10 d10 d01 a00 d11 e0 a10 r1 c0 t0 n01 c1 n11 j0 v0 e1 t1 s0 j1 s1 v1",
       "d00 n00 d10 n10 d01 A00 A01 d11 A02 A03 e0 t0 n01 A10 A11 N11 A12 j0 A13 v0 e1 t1 s0 j1 s1 v1",
       "d00 n00 d10 n10 d01 A00 A01 d11 A02 A03 e0 t0 n01 A10 A11 N11 A12 j0 A13 v0 e1 t1 s0 j1 s1 v1"]
GS = [0, 512]
ALT = [1]
SEMAPHORES = ["cv", "cs", "cp", "cg", "sent"] + ["d%d" % i for i in range(NDMA)] + ["a%d" % i for i in range(8)]
A = AluOpType
ACT = ActivationFunctionType


def rank_program(g, core, T, topo):
    rank = T.rank_of(core)
    if rank is None:
        return
    n = len(T.cores)
    nxt, prv = T.cores[(rank + 1) % n], T.cores[(rank - 1) % n]
    assert topo.may_write(core, nxt)
    rid, pid = topo.addr(nxt)[:2]
    eng_out, eng_in = topo.engines(core, nxt), topo.engines(prv, core)
    Q = {"v": g.vector, "s": g.scalar, "p": g.tensor, "g": g, "y": g.sync}
    CS = {"v": "cv", "s": "cs", "p": "cp", "g": "cg"}
    count = {}
    seen = {q: {} for q in Q}
    hist = {}
    ndma = [0]
    nsend = [0]

    def ap(name, lo=0, hi=None, step=None):
        if hi is None:
            hi = SCRATCH[name][1][1]
        a = T[name][:, lo:hi] if step is None else T[name][:, lo:hi:step]
        return (a, [(name, lo, hi)])

    def ind(win, off):
        return (win[0].indirect(off[0]), win[1] + off[1])

    def need(q, sem, val):
        if seen[q].get(sem, 0) < val:
            Q[q].wait_ge(T.sem[sem], val)
            seen[q][sem] = val

    def order(q, reads, writes):
        want = {}
        for rs, w in ((reads, False), (writes, True)):
            for name, lo, hi in rs:
                psum = SCRATCH[name][0] == "psum"
                for l2, h2, w2, q2, sem, val in hist.get(name, []):
                    if (psum and q2 != q) or ((w or w2) and l2 < hi and lo < h2):
                        want[sem] = max(want.get(sem, 0), val)
        for sem in want:
            need(q, sem, want[sem])

    def note(q, reads, writes, sem, val):
        for rs, w in ((reads, False), (writes, True)):
            for name, lo, hi in rs:
                h = hist.setdefault(name, [])
                if w:
                    h[:] = [x for x in h if not (lo <= x[0] and x[1] <= hi)]
                h.append((lo, hi, w, q, sem, val))

    def regs(xs):
        out = []
        for x in xs:
            if isinstance(x, tuple):
                out += x[1]
        return out

    def raw(x):
        return x[0] if isinstance(x, tuple) else x

    def run(q, out, ins, calls, each=False, wait=True):
        r, w = regs(ins), out[1]
        order(q, r, w if wait else [])
        sem = CS[q]
        for i, c in enumerate(calls):
            inst = c()
            if each or i == len(calls) - 1:
                inst.then_inc(T.sem[sem], 1)
                count[sem] = count.get(sem, 0) + 1
        note(q, r, w, sem, count[sem])

    def cp(out, x):
        run("v", out, [x], [lambda: g.vector.tensor_copy(out[0], x[0])])

    def tt(out, x, y, op):
        run("v", out, [x, y], [lambda: g.vector.tensor_tensor(out[0], x[0], y[0], op)])

    def ts(out, x, s1, op0, s2=None, op1=None):
        if op1 is None:
            run("v", out, [x, s1], [lambda: g.vector.tensor_scalar(out[0], x[0], raw(s1), None, op0)])
        else:
            run("v", out, [x, s1, s2], [lambda: g.vector.tensor_scalar(out[0], x[0], raw(s1), raw(s2), op0, op1)])

    def ms(out, c):
        run("v", out, [], [lambda: g.vector.memset(out[0], c)])

    def act(out, x, func=ACT.Identity, **kw):
        k2 = {k: raw(kw[k]) for k in kw}
        run("s", out, [x] + list(kw.values()), [lambda: g.scalar.activation(out[0], x[0], func, **k2)])

    def iota(out, pattern, base, cm):
        if SCRATCH[out[1][0][0]][2] == I32:
            run("g", out, [], [lambda: g.iota(out[0], pattern, base, cm)])
        else:
            run("g", out, [], [lambda: g.iota(out[0], pattern, base, cm, allow_small_or_imprecise_dtypes=True)])

    def gcopy(out, x):
        m = out[1][0][2] - out[1][0][1]
        run("g", out, [x], [lambda: g.affine_select(out[0], x[0], [[0, m]], A.is_ge, 0.0, 0, 0)])

    def dma(q, out, x, **kw):
        r, w = regs([x]), regs([out])
        order(q, r, w)
        sem = "d%d" % ndma[0]
        ndma[0] += 1
        Q[q].dma_start(raw(out), raw(x), **kw).then_inc(T.sem[sem], 16)
        count[sem] = 16
        note(q, r, w, sem, 16)

    def twin(dst, src, lo, hi, j):
        m = lo + GS[j]
        if m > lo:
            gcopy(ap(dst, lo, m), ap(src, lo, m))
        if m < hi:
            dma("y", ap(dst, m, hi), ap(src, m, hi))

    def send(srcs, dst):
        sem = "a%d" % nsend[0]
        nsend[0] += 1
        order("g", regs(srcs), [])
        if len(srcs) == 1:
            g.remote_dma(dst[0], srcs[0][0], T.sem[sem], T.sem.sent, pid, rid, topo.mask(core, nxt))
        else:
            g.remote_dma_fused([RemoteDMATransfer(dst_ids=[DstId(rid=rid, pnc=pid)], dma_engine_mask=topo.mask(core, nxt), remote_sem=T.sem[sem],
                                                  srcs=[x[0] for x in srcs], dsts=[dst[0]], alu_op=1)], local_sem=T.sem.sent)
        count["sent"] = count.get("sent", 0) + len(eng_out)
        count[sem] = len(eng_in)
        note("r", [], dst[1], sem, len(eng_in))

    def extract(out, sel, src, lo, hi):
        run("p", out, [ap(sel), ap(src, lo, hi)],
            [lambda i=i: g.tensor.matmul(out[0], T[sel][:, 15 - i:143 - i], T[src][:, lo + i:hi:16], i == 0, i == 15) for i in range(16)])

    dma("y", ap("sndi"), T.snd[:])
    dma("s", ap("phr", 0, H), T.phi[:, 0:H])
    dma("y", ap("phr", H, V), T.phi[:, H:V])
    dma("s", ap("nl", 0, 128), T.nb[0:8:2, :])
    dma("y", ap("nl", 128, 256), T.nb[1:8:2, :])
    iota(ap("xj"), [[-1, 8]], 16, 1)
    iota(ap("h64"), [[64, 17]], 0, 0)
    iota(ap("lo64"), [[1, 64]], 0, 0)
    iota(ap("xg"), [[-16, 8]], 0, 1)
    iota(ap("pa"), [[16, 8], [128, 2]], 0, 0)
    iota(ap("pb"), [[2, 16]], 0, 0)
    iota(ap("c16"), [[16, 128]], 0, 0)
    iota(ap("one"), [[0, 128]], 1, 0)
    run("g", ap("idf"), [ap("one")], [lambda: g.affine_select(T.idf[:, :], T.one[:, :], [[-1, 128]], A.is_equal, 0.0, 0, 1)])
    ms(ap("neg", 0, 1), -0.5)
    ms(ap("neg", 1, 2), -1.0)
    ms(ap("neg", 2, 3), (rank + 1) / 4.0)
    for name in ("fb", "fp", "f0", "f5"):
        ms(ap(name), 0.0)
    ts(ap("ya"), ap("xj", 2, 4), 11, A.bitwise_and)
    ts(ap("yb"), ap("xj"), 15, A.bitwise_and)
    ts(ap("abc"), ap("ya"), 0.0, A.is_equal)
    ts(ap("eq"), ap("yb"), 0.0, A.is_equal)
    ts(ap("cc"), ap("yb", 7, 8), 0.0, A.is_equal, (rank + 1) / 4.0, A.mult)
    ts(ap("at"), ap("h64"), ap("abc", 0, 1), A.mult)
    ts(ap("yy", 0, 64), ap("lo64"), ap("abc", 1, 2), A.mult, ap("cc"), A.add)
    ts(ap("yc"), ap("xj", 0, 1), 7, A.bitwise_and)
    act(ap("m0"), ap("eq", 2, 3), scale=float(V))
    act(ap("ata"), ap("h64"), scale=ap("eq", 2, 3))
    act(ap("m23"), ap("eq", 6, 7), bias=ap("eq", 7, 8))
    act(ap("posg", 0, 64), ap("lo64"), scale=ap("eq", 3, 4), bias=ap("m0"))
    for k in range(3):
        act(ap("posg", 64 << k, 128 << k), ap("posg", 0, 64 << k), bias=ap("ata", 1 << k, (1 << k) + 1))
    for k in range(5):
        ts(ap("yy", 64 << k, 128 << k), ap("yy", 0, 64 << k), ap("at", 1 << k, (1 << k) + 1), A.add)
        if k == 0:
            cp(ap("pf", 0, 1), ap("yb", 0, 1))
            cp(ap("pf", 1, 2), ap("yc"))
        if k == 1:
            ts(ap("pau"), ap("pa"), ap("pf", 0, 1), A.add)
            ts(ap("pf", 2, 3), ap("pf", 1, 2), 31.875, A.mult)
        if k == 2:
            ts(ap("pf", 3, 4), ap("pf", 0, 1), 0.125, A.mult, ap("pf", 2, 3), A.add)
            ts(ap("x2"), ap("xg"), 1, A.arith_shift_right)
        if k == 3:
            ts(ap("pbu"), ap("pb"), ap("pf", 3, 4), A.add)
            ts(ap("x16"), ap("xg"), 4, A.arith_shift_right)
    cp(ap("snl"), ap("sndi"))
    act(ap("vw"), ap("c16"), bias=ap("pf", 0, 1))
    act(ap("oneb"), ap("one", 0, 64))
    act(ap("nr"), ap("vw"), bias=ap("neg", 2, 3))
    act(ap("sp"), ind(ap("phr"), ap("snl")), scale=1.0 / 256, bias=ap("neg", 0, 1))
    send([ap("sp")], ap("phw", V, W))
    act(ap("sm1"), ind(ap("yy", 0, V), ap("snl")), scale=ap("m23"))
    send([ap("sm1"), ap("posg")], ap("yy", V, W))
    ts(ap("x8"), ap("xg"), 0x7FF7, A.bitwise_and)
    ts(ap("fb", 15, 143, 16), ap("x2"), 3.0, A.is_equal)
    ts(ap("fp", 15, 143, 16), ap("x2"), 1.0, A.is_equal)
    for j, c in enumerate((UNIT, 2 * UNIT, -UNIT)):
        ts(ap("gob", 8 * j, 8 * j + 8), ap("x16"), 0.0, A.is_equal, c, A.mult)
    ts(ap("gof"), ap("x16"), 0.0, A.is_equal, UNIT, A.mult)
    ts(ap("f0", 15, 143, 16), ap("x8"), 1.0, A.is_equal)
    ts(ap("f5", 15, 143, 16), ap("x8"), 5.0, A.is_equal)
    for h in range(2):
        ts(ap("phw", H * h, H * h + H), ap("phr", H * h, H * h + H), 128.0, A.subtract, 1.0 / 256, A.mult)
        dma("y", ap("phs", H * h, H * h + H), ap("phw", H * h, H * h + H))
    cp(ap("nl2"), ind(ap("nl"), ap("pau")))
    cp(ap("nh"), ap("nl"))
    run("v", ap("nl3"), [ap("nl2")], [lambda: g.vector.transpose(T.nl3[:, :], T.nl2[:, :])])
    tt(ap("rpm"), ap("idf", 0, 64), ap("idf", 64, 128), A.subtract)
    cp(ap("ul"), ind(ap("nl3"), ap("pbu")))
    for j in range(4):
        act(ap("vw2", 64 * j, 64 * j + 64), ap("vw", 64 * (j // 2), 64 * (j // 2) + 64))
    act(ap("idn"), ap("idf"), scale=-BIG)
    act(ap("idp"), ap("idf"), scale=BIG)
    act(ap("idb"), ap("idf"))
    tt(ap("nlo"), ap("nl"), ap("nh"), A.subtract)
    for h in range(2):
        ts(ap("top", 128 * h, 128 * h + 128), ap("vw2", 128 * h, 128 * h + 128), float(W + H * h + H), A.add)
    for name, lo, hi in (("w1", 0, W), ("ki", V, W), ("ka", V, W), ("kb", V, W), ("wd2", 0, 16), ("wd3", 0, 16)):
        iota(ap(name, lo, hi), [[0, hi - lo]], 0, 0)
    dma("y", ap("z0", V, W), ap("yy", V, W))
    for c in range(4):
        j0 = 4 * (c // 2) + 2 * (c % 2)
        dma("y", (T.sd[:, j0:j0 + 2, :], [("sd", j0, j0 + 2)]), ap(("nh", "nlo")[c % 2], 128 * (c // 2), 128 * (c // 2) + 128))

    for rnd in range(3):
        x = "z%d" % rnd
        znext = "z%d" % (rnd + 1)
        uw = ("phw", "w2", "w3")[rnd]
        dw = ("w1", "w2", "w3")[rnd]
        ul = ("ul", "ul", "ul2")[rnd]
        ab = (("ac0", "ac1"), ("ab0", "ab1"), ("ab0", "ab1"))[rnd]
        go = (ap("gob", 0, 8), ap("gof"), ap("gof"))[rnd]
        nq = "nq" if rnd else "nr"
        wide = 128 if rnd == 1 else 64
        relu = {}

        def col(k, h):
            return W + V * h + H * k

        def dk(k, h):
            l0, lo = 128 * k + 64 * h, col(k, h)
            w = ind(ap(uw, 0, W), ap(ul, l0, l0 + 64))
            if rnd == 1:
                tt(ap(dw, lo, lo + H), w, ap("w1", lo, lo + H), A.add)
            else:
                tt(ap(dw, lo, lo + H), w, ap("us" if rnd else "phs", H * h, H * h + H), A.subtract)

        def nk(k, h, f=act):
            lo, l0 = col(k, h), 128 * k + 64 * h
            f(ap("yy", lo, lo + H), ind(ap("yy", 0, W), ap(ul, l0, l0 + 64)))
            extract(ap("dec%d" % h, 64 * k, 64 * k + 64), "fb", "yy", lo, lo + H)

        def absk(k, h):
            act(ap(ab[h], H * k, H * k + H), ap(dw, col(k, h), col(k, h) + H), ACT.Abs)

        def absq(h, r):
            lo, tp = col(0, h), "tp%d" % h
            act(ap(ab[h], QN * r, QN * r + QN), ap(dw, lo + r, lo + V, 4), ACT.Abs)
            run("p", ap(tp, r, 128), [ap(ab[h], QN * r, QN * r + QN), go],
                [lambda i=i: g.tensor.matmul(T[tp][:, 4 * i + r:128:16], T[ab[h]][:, QN * r + i:QN * r + QN:4], go[0], True, True) for i in range(4)],
                each=True, wait=r == 0)

        def pos(h):
            relu[h] = 1
            ts(ap(ab[h]), ap(dw, col(0, h), col(0, h) + V), 0.0, A.max)

        def cost1(h):
            tp, lo = "tp%d" % h, col(0, h)
            if h not in relu:
                run("p", ap(tp, 0, 128), [ap(ab[h]), go],
                    [lambda i=i: g.tensor.matmul(T[tp][:, i:128:16], T[ab[h]][:, i:V:16], go[0], True, True) for i in range(16)], each=True)
            else:
                calls = []
                for i in range(16):
                    calls += [lambda i=i: g.tensor.matmul(T[tp][:, i:128:16], T[dw][:, lo + i:lo + V:16], T.gob[:, 16:24], True, False),
                              lambda i=i: g.tensor.matmul(T[tp][:, i:128:16], T[ab[h]][:, i:V:16], T.gob[:, 8:16], False, True)]
                run("p", ap(tp, 0, 128), [ap(ab[h]), ap(dw, lo, lo + V), ap("gob")], calls, each=True)

        def may(h):
            e, d, c = "ea%d" % h, "dec%d" % h, ap(nq, 64 * h, 64 * h + 64)
            for k in range(2):
                tt(ap(e, 128 * k, 128 * k + 64), ap(d, 64 * k, 64 * k + 64), c, A.is_lt)
                if rnd == 1:
                    tt(ap(e, 128 * k + 64, 128 * k + 128), ap(d, 64 * k, 64 * k + 64), c, A.is_le)
            o = (128 * h, 128 * h + wide)
            ts(ap("bs", *o), ap(e, 0, wide), float(W + H * h), A.mult)
            terms = [[("idn", ap("oneb")), ("idn", ap(e, 0, 64)), ("idp", ap(e, 128, 192)), ("idp", ap(e, 128, 192))]]
            if rnd == 1:
                terms.append([("idn", ap("oneb")), ("idn", ap(e, 0, 64)), ("idn", ap(e, 64, 128)), ("idp", ap(e, 128, 192)),
                              ("idp", ap(e, 192, 256)), ("idp", ap(e, 192, 256))])
            for z, tm in zip((ap(d, 128, 192), ap("pp%d" % h, 128, 192)), terms):
                run("p", z, [ap("idn"), ap("idp")] + [y[1] for y in tm],
                    [lambda i=i, z=z, tm=tm: g.tensor.matmul(z[0], T[tm[i][0]][:, :], tm[i][1][0], i == 0, False) for i in range(len(tm))])
            tt(ap("bt", *o), ap("bs", *o), ap("vw2", *o), A.add)

        def cost2(h):
            cp(ap("ts%d" % h), ap("tp%d" % h, 0, 128))
            for z in (ap("dec%d" % h, 128, 192), ap("pp%d" % h, 128, 192))[:wide // 64]:
                run("p", z, [ap("ts%d" % h), ap("rpm")],
                    [lambda z=z: g.tensor.matmul(z[0], T["ts%d" % h][:, :], T.rpm[:, :], False, True)], wait=False)

        def decide(h):
            o = (128 * h, 128 * h + wide)
            tt(ap("by", o[0], o[0] + 64), ap("dec%d" % h, 128, 192), ap("bt", o[0], o[0] + 64), A.max)
            if rnd == 1:
                tt(ap("by", o[0] + 64, o[1]), ap("pp%d" % h, 128, 192), ap("bt", o[0] + 64, o[1]), A.max)
            tt(ap("bz", *o), ap("by", *o), ap("top", *o), A.min)
            cp(ap("bl", *o), ap("bz", *o))

        def picks(h):
            o = 128 * h + wide - 64
            act(ap(x, H * h, H * h + H), ind(ap("yy", 0, col(0, h) + V), ap("bl", o, o + 64)))
            extract(ap("pp%d" % h, 0, 64), "fp", x, H * h, H * h + H)

        def pickv(h):
            for j in range(2):
                lo = H * h + QN * j
                if h == 1 and j == 1:
                    cp(ap("pl0", 0, 64), ap("pp0", 0, 64))
                ts(ap("ki", lo, lo + QN), ind(ap(dw, 0, col(0, h) + V), ap("bl", 128 * h + 32 * j, 128 * h + 32 * j + 32)), 1.0 / 512, A.add)
                twin("kd", "ki", lo, lo + QN, j)

        steps = {"d": dk, "n": nk, "N": lambda k, h: nk(k, h, cp), "a": absk, "A": absq, "r": pos, "c": cost1, "e": may, "t": cost2,
                 "j": decide, "v": pickv, "s": picks}
        if rnd == 1:
            dma("g", ap("ou"), ap("sp"))
            dma("g", ap("ou"), ap("sk2"), accum_op=A.add)
        for w in SEQ[rnd].split():
            steps[w[0]](*[int(z) for z in w[1:]])
        ksrc = ["ki", "ka", "kb", "ka", "kb"]
        nsrc = [x, "yy", x, "yy", znext]
        if rnd == 1:
            extract(ap("xa", 0, 128), "f0", x, 0, V)

        def narrow(t, lo, hi):
            act(ap(nsrc[t + 1], lo, hi), ind(ap(nsrc[t], 0, W), ap("pl%d" % (t % 2), lo // 16, hi // 16)))
            extract(ap("pp%d" % (lo // H), lo % H // 16, lo % H // 16 + (hi - lo) // 16), "fp", nsrc[t + 1], lo, hi)

        def broad(t, lo, hi):
            tt(ap(ksrc[t + 1], lo, hi), ind(ap(ksrc[t]), ap("pl%d" % (t % 2), lo // 16, hi // 16)), ap("tt" if t else "kd", lo, hi), A.add)

        def quarter(t, h, j):
            return H * h + QN * (j ^ (ALT[0] & (t + 1) & 1))

        def lists(lo, hi, base):
            p, c = ap("pp%d" % (lo // H), lo % H // 16, lo % H // 16 + (hi - lo) // 16), (lo // 16, hi // 16)
            tt(ap("lf", *c), p, ap("vw", *c), A.max)
            ts(ap("lg", *c), p, float(V - 16), A.subtract, 0.0, A.max)
            ts(ap("ll", *c), ap("lf", *c), float(base), A.subtract)

        def roots(h):
            c = (64 * h, 64 * h + 64)
            tt(ap("rt", *c), ap("pp%d" % h, 0, 64), ap("vw", *c), A.is_equal)
            tt(ap("nq", *c), ap("rt", *c), ap("nr", *c), A.mult)

        for t in range(3):
            for h in range(2):
                narrow(t, H * h, H * h + H)
                if rnd == 1 and t == 0 and h == 0:
                    extract(ap("xb", 0, 128), "f5", x, 0, V)
                for j in range(2):
                    lo = quarter(t, h, j)
                    if j == 1:
                        cp(ap("pl%d" % ((t + h) % 2), 64 - 64 * h, 128 - 64 * h), ap("pp%d" % (1 - h), 0, 64))
                    broad(t, lo, lo + QN)
                    twin("tt", ksrc[t + 1], lo, lo + QN, j)
                if rnd == 1 and t == 1:
                    cp(ap("ul2", 128 * h, 128 * h + 128), ap(("xa", "xb")[h], 0, 128))
        if rnd == 0:
            act(ap("e8"), ind(ap("yy", 0, V), ap("snl")))
            extract(ap("xa", 0, 32), "fp", "e8", 0, G)
            cp(ap("pl1", 64, 128), ap("pp1", 0, 64))
            cp(ap("f1"), ind(ap("ka", 0, V), ap("snl")))
            narrow(3, 3 * QN, V)
            cp(ap("el"), ap("xa", 0, 32))
            tt(ap("sk2"), ind(ap("ka"), ap("el")), ap("f1"), A.add)
            send([ap("sk2")], ap("wd2", 16, 16 + G))
            act(ap("sm2"), ind(ap("yy", 0, W), ap("el")), scale=ap("m23"))
            send([ap("sm2"), ap("posg")], ap("z1", V, W))
            gcopy(ap("w2", V, W), ap("wd2", 16, 16 + G))
            for j in range(4):
                q = 3 - j
                if j:
                    narrow(3, QN * q, QN * q + QN)
                dma("y", (T.z1[1:128:4, QN * q:QN * q + QN], [("z1", QN * q, QN * q + QN)]), (T.sd[:, :, QN * q:QN * q + QN], [("sd", 0, 8)]))
            for j in range(4):
                lo = quarter(3, j // 2, j % 2)
                broad(3, lo, lo + QN)
                if j >= 2:
                    lists(QN * (5 - j), QN * (6 - j), QN * (5 - j))
            gcopy(ap("yy", V, W), ap("z1", V, W))
            for j in range(4):
                q = 3 - j
                act(ap("yy", QN * q, QN * q + QN), ind(ap("z1", QN * q, W), ap("ll", 32 * q, 32 * q + 32)))
                if j == 0:
                    lists(QN, H, QN)
                    lists(0, QN, 0)
                if j % 2 == 0:
                    h = q // 2
                    tt(ap("w2", H * h, H * h + H), ind(ap("wd2"), ap("lg", 64 * h, 64 * h + 64)), ap("kb", H * h, H * h + H), A.add)
                    roots(h)
        elif rnd == 1:
            def usum(j):
                lo, b = quarter(3, j // 2, j % 2), ("xa", "xb")[j % 2]
                run("p", ap(b), [ap("idb"), ap("idf"), ap("phs", lo, lo + QN), ap("kb", lo, lo + QN)],
                    [lambda: g.tensor.matmul(T[b][:, :], T.idb[:, :], T.phs[:, lo:lo + QN], True, False),
                     lambda: g.tensor.matmul(T[b][:, :], T.idf[:, :], T.kb[:, lo:lo + QN], False, True)])

            def uout(j):
                lo = quarter(3, j // 2, j % 2)
                act(ap("uo", lo, lo + QN), ap(("xa", "xb")[j % 2]))

            narrow(3, 0, H)
            broad(3, quarter(3, 0, 0), quarter(3, 0, 0) + QN)
            usum(0)
            cp(ap("pl1", 64, 128), ap("pp1", 0, 64))
            narrow(3, H, V)
            for j in range(1, 4):
                lo = quarter(3, j // 2, j % 2)
                broad(3, lo, lo + QN)
            usum(1)
            act(ap("sm3"), ind(ap("z2", 0, V), ap("snl")), scale=ap("m23"))
            send([ap("sm3"), ap("posg")], ap("z2", V, W))
            tt(ap("sk3"), ind(ap("kb", 0, V), ap("snl")), ap("sk2"), A.subtract)
            send([ap("sk3")], ap("wd3", 16, 16 + G))
            send([ap("sk3"), ap("ou")], ap("w3", V, W))
            uout(0)
            usum(2)
            uout(1)
            usum(3)
            uout(2)
            for h in range(2):
                lists(H * h, H * h + H, 0)
                roots(h)
                tt(ap("us", H * h, H * h + H), ind(ap("w2"), ap("bl", 128 * h + 64, 128 * h + 128)), ap("phs", H * h, H * h + H), A.add)
            gcopy(ap("yy", V, W), ap("z2", V, W))
            for h in range(2):
                act(ap("yy", H * h, H * h + H), ind(ap("z2"), ap("ll", 64 * h, 64 * h + 64)))
                if h == 0:
                    uout(3)
                tt(ap("w3", H * h, H * h + H), ind(ap("wd3"), ap("lg", 64 * h, 64 * h + 64)), ap("uo", H * h, H * h + H), A.add)
        else:
            for h in range(2):
                for lo, hi in ((0, H),) if h == 0 else ((H, H + 768), (H + 768, V)):
                    act(ap("z3", lo, hi), ind(ap("yy", 0, W), ap("pl1", lo // 16, hi // 16)))
                    run("p", ap("xa", 0, 128), [ap("fb"), ap("z3", lo, hi)],
                        [lambda i=i: g.tensor.matmul(T.xa[:, 0:128], T.fb[:, 15 - i:143 - i], T.z3[:, 128 * i:128 * i + 128], i == 0, i == 15)
                         for i in range(lo // 128, hi // 128)], wait=lo == 0)
                for j in range(2):
                    lo = quarter(3, h, j)
                    if j == 1 and h == 0:
                        cp(ap("pl1", 64, 128), ap("pp1", 0, 64))
                    for a, b in ((lo, lo + QN // 2), (lo + QN // 2, lo + QN)) if h == 1 and j == 1 else ((lo, lo + QN),):
                        broad(3, a, b)
                        dma("y", T.yk[:, a:b], ap("kb", a, b))
    act(ap("yrs"), ap("xa", 0, 128), scale=4.0, bias=ap("neg", 1, 2))
    dma("s", T.yr[:], ap("yrs"))
    for sem in count:
        need("g", sem, count[sem])
